import numpy as np
import ml_dtypes


def mxq(x, axis, fmt="e4m3"):
    dtype, down = {"e4m3": (ml_dtypes.float8_e4m3fn, 7), "e5m2": (ml_dtypes.float8_e5m2, 14)}[fmt]
    v = np.moveaxis(np.asarray(x, np.float32).astype(ml_dtypes.bfloat16).astype(np.float64), axis, -1)
    blocks = v.reshape(v.shape[:-1] + (-1, 32))
    amax = np.abs(blocks).max(-1, keepdims=True)
    byte = np.maximum(np.where(amax > 0, np.frexp(amax)[1] - 1 + 127, 0) - down, 1)
    scale = np.exp2(byte - 127.0)
    codes = (blocks / scale).astype(np.float32).astype(dtype).astype(np.float64)
    return np.moveaxis((codes * scale).reshape(v.shape), -1, axis)


WIDE = False


def mx_kscale(k):
    if not WIDE:
        return np.ones(k)
    levels = np.array([10, -10, 5, -5, 0])
    if k % 512:
        return np.exp2(np.random.permutation(np.resize(levels, k // 32))).repeat(32)
    a = np.empty((k // 512, 16))
    for p in range(k // 512):
        a[p, :8] = np.random.permutation(np.resize(levels, 8))
        for g in range(8):
            far = levels[np.abs(levels - a[p, g]) >= 10]
            a[p, g + 8] = far[np.random.randint(len(far))]
    return np.exp2(a.ravel()).repeat(32)


def f64(x):
    return np.asarray(x).astype(np.float64)


def striped(idx):
    return np.tile(idx.reshape(-1, 16).T, (8, 1)).astype(np.uint16)


def unstriped(offs):
    return offs[:16].T.reshape(-1).astype(np.int64)


E2M1 = np.array([0.0, 0.5, 1.0, 1.5, 2.0, 3.0, 4.0, 6.0, -0.0, -0.5, -1.0, -1.5, -2.0, -3.0, -4.0, -6.0])


def pack_weight(w, fmt):
    k, n = w.shape
    w = f64(np.asarray(w, np.float32).astype(ml_dtypes.bfloat16)).reshape(k // 32, 32, n)
    amax = np.abs(w).max(1)
    if fmt == "e4m3":
        byte = np.frexp(amax)[1] - 1 + 127 - 7
    else:
        mant, ex = np.frexp(amax / 6.0)
        byte = np.where(mant > 0.5, ex, ex - 1) + 127
    byte = np.clip(np.where(amax > 0, byte, 1), 1, 254)
    scaled = (w * np.exp2(127.0 - byte)[:, None, :]).reshape(k, n).astype(np.float32)
    by_word = np.ascontiguousarray(scaled.reshape(k // 512, 128, 4, n).transpose(0, 1, 3, 2))
    if fmt == "e4m3":
        words = by_word.astype(ml_dtypes.float8_e4m3fn).view(np.uint8)
    else:
        c = by_word.astype(ml_dtypes.float4_e2m1fn).view(np.uint8) & 0xF
        words = (c[..., 0::2] | (c[..., 1::2] << 4)).reshape(k // 512, 128, 2 * n)
    return np.ascontiguousarray(words), np.ascontiguousarray(byte.astype(np.uint8).reshape(k // 512, 16, n))


def unpack_weight(words, scales, fmt):
    g, _, n = scales.shape
    words = np.ascontiguousarray(words).reshape(g, 128, n, -1)
    if fmt == "e4m3":
        vals = words.view(ml_dtypes.float8_e4m3fn).astype(np.float64)
    else:
        nib = np.empty((g, 128, n, 4), np.uint8)
        nib[..., 0::2] = words & 0xF
        nib[..., 1::2] = words >> 4
        vals = E2M1[nib]
    vals = vals * np.repeat(np.exp2(scales.astype(np.float64) - 127.0), 8, axis=1)[..., None]
    return vals.transpose(0, 1, 3, 2).reshape(g * 512, n)


def gelu(v):
    return 0.5 * v * (1.0 + np.tanh(np.sqrt(2.0 / np.pi) * (v + 0.044715 * v**3)))


K, H, T, S, T2, S2 = 1024, 512, 2048, 1024, 1024, 512


def setup_inputs():
    n = np.random.standard_normal
    s = mx_kscale(K)[:, None]
    u = mx_kscale(H)[:, None]
    tab_words, tab_scales = pack_weight(n((K, T)) * s, "e4m3")
    tab2_words, tab2_scales = pack_weight(1.2 * n((H, T2)) / np.sqrt(H) / u, "e4m3")
    w4_words, w4_scales = pack_weight(0.9 * n((K, H)) / np.sqrt(K) / s * u.T, "e2m1")
    return {
        "tab_words": tab_words, "tab_scales": tab_scales,
        "offs": striped(np.random.permutation(T)[:S]),
        "tab2_words": tab2_words, "tab2_scales": tab2_scales,
        "offs2": striped(np.random.permutation(T2)[:S2]),
        "w4_words": w4_words, "w4_scales": w4_scales,
        "w1": (0.5 * n((K, H)) / np.sqrt(K) / s * u.T).astype(np.float32),
        "b1": (0.4 * n(H) * u[:, 0]).astype(np.float32),
        "temp": np.exp(0.2 * n(S)).astype(np.float32),
    }


def reference(tab_words, tab_scales, offs, tab2_words, tab2_scales, offs2, w4_words, w4_scales, w1, b1, temp):
    v = unpack_weight(tab_words, tab_scales, "e4m3")[:, unstriped(offs)]
    v2 = unpack_weight(tab2_words, tab2_scales, "e4m3")[:, unstriped(offs2)]
    w4 = unpack_weight(w4_words, w4_scales, "e2m1")
    w1q = mxq(f64(w1), 0, "e4m3")
    h = (w4.T @ v + w1q.T @ v) + f64(b1)[:, None]
    hq = mxq(h, 0, "e4m3")
    z = (v2.T @ hq) * f64(temp)[None, :]
    return np.sqrt(np.log1p(np.exp(z)))

@@ -1,0 +1,241 @@
+from contextlib import ExitStack
+
+import concourse.mybir as mybir
+from concourse.masks import make_identity
+
+K, H, T, S, T2, S2 = 1024, 512, 2048, 1024, 1024, 512
+FLOPS = 2 * (2 * K * H * S + H * S2 * S)
+
+F32 = mybir.dt.float32
+BF16 = mybir.dt.bfloat16
+I32 = mybir.dt.int32
+U32 = mybir.dt.uint32
+U16 = mybir.dt.uint16
+U8 = mybir.dt.uint8
+FP8X4 = mybir.dt.float8_e4m3fn_x4
+FP4X4 = mybir.dt.float4_e2m1fn_x4
+ACT = mybir.ActivationFunctionType
+ALU = mybir.AluOpType
+
+P = 128
+PACK = 4
+PASSES = K // (P * PACK)
+BANK = 512
+HALVES = S // BANK
+TILES = S // P
+PAIR = 2 * P
+LN_FLOOR = 2.0**-60
+SQRT_FLOOR = 2.0**-100
+VECTOR_PLANES = []
+
+
+def tile_list_expert_routing_affinities_kernel(
+    tc, tab_words, tab_scales, offs, tab2_words, tab2_scales, offs2, w4_words, w4_scales, w1, b1, temp, out
+):
+    nc = tc.nc
+    with ExitStack() as ctx:
+        lists = ctx.enter_context(tc.tile_pool(name="lists", bufs=1))
+        keep = ctx.enter_context(tc.tile_pool(name="keep", bufs=1))
+        psum = ctx.enter_context(tc.psum_pool(name="psum", bufs=1))
+
+        def sb(name, shape, dtype):
+            return keep.tile(shape, dtype, name=name, align_bytes=64)
+
+        def bank(name, b):
+            return psum.tile([P, BANK], F32, name=name, tag="bank%d" % b)
+
+        tokens = lists.tile([P, S // 16], U16, name="tokens")
+        experts = lists.tile([P, S2 // 16], U16, name="experts")
+        v_scale_tab = sb("v_scale_tab", [P, PASSES, T // 4], I32)
+        w4_scale_raw = sb("w4_scale_raw", [P, PASSES, H // 4], I32)
+        c_scale_tab = sb("c_scale_tab", [P, T2 // 4], I32)
+        temp_rows = sb("temp_rows", [P, P], F32)
+        bias = sb("bias", [P, PACK], F32)
+        w4_raw = sb("w4_raw", [P, PASSES, H // 2], I32)
+        w1_raw = [sb("w1_raw%d" % a, [P, PACK, H], F32) for a in range(PASSES)]
+        v_word_tab = [sb("v_word_tab%d" % a, [P, T], I32) for a in range(PASSES)]
+        c_word_tab = sb("c_word_tab", [P, T2], I32)
+        ident = sb("ident", [P, P], F32)
+        warm = sb("warm", [P, 2], F32)
+
+        nc.vector.memset(v_scale_tab[:], 0)
+        nc.vector.memset(w4_scale_raw[:], 0)
+        nc.gpsimd.memset(temp_rows[:], 0.0)
+        nc.gpsimd.dma_start(out=temp_rows[0:TILES, :], in_=temp.rearrange("(i p) -> i p", p=P))
+        nc.gpsimd.dma_start(out=bias[:], in_=b1.rearrange("(p t) -> p t", t=PACK))
+        make_identity(nc, ident[:])
+        nc.gpsimd.memset(c_scale_tab[:], 0)
+        nc.scalar.activation(out=warm[:, 0:1], in_=ident[:, 0:1], func=ACT.Sigmoid)
+
+        def load_scale_rows(engine, plane, rows_of):
+            for quad in range(4):
+                engine.dma_start(out=plane(slice(32 * quad, 32 * quad + 4)), in_=rows_of(slice(4 * quad, 4 * quad + 4)).bitcast(I32))
+
+        def load_w1(a):
+            nc.sync.dma_start(out=w1_raw[a][:], in_=w1[512 * a : 512 * (a + 1), :].rearrange("(p j) c -> p j c", j=PACK))
+
+        def load_v(a):
+            nc.sync.dma_start(out=v_word_tab[a][:], in_=tab_words[a].rearrange("p t i -> p (t i)").bitcast(I32))
+
+        nc.sync.dma_start(tokens[:], offs)
+        nc.sync.dma_start(out=w4_raw[:], in_=w4_words.rearrange("a p n -> p a n").bitcast(I32))
+        load_scale_rows(nc.sync, lambda live: v_scale_tab[live, :, :], lambda rows: tab_scales[:, rows, :].rearrange("a r n -> r a n"))
+        load_w1(0)
+        load_v(0)
+        load_scale_rows(nc.sync, lambda live: w4_scale_raw[live, :, :], lambda rows: w4_scales[:, rows, :].rearrange("a r n -> r a n"))
+        load_w1(1)
+        load_v(1)
+        nc.sync.dma_start(experts[:], offs2)
+        nc.sync.dma_start(out=c_word_tab[:], in_=tab2_words[0].rearrange("p t i -> p (t i)").bitcast(I32))
+        load_scale_rows(nc.gpsimd, lambda live: c_scale_tab[live, :], lambda rows: tab2_scales[0, rows, :])
+
+        w4_codes = sb("w4_codes", [P, PASSES, 2 * H], U8)
+        w4_planes = sb("w4_planes", [P, PASSES, H], U8)
+        nc.vector.tensor_copy(
+            out=w4_planes[:].rearrange("p a (t m) -> p a t m", t=PACK),
+            in_=w4_scale_raw[:].bitcast(U8).rearrange("p a (m t) -> p a t m", t=PACK),
+        )
+        nc.vector.tensor_copy(
+            out=w4_codes[:].bitcast(U16).rearrange("p a (t m) -> p a t m", t=PACK),
+            in_=w4_raw[:].bitcast(U16).rearrange("p a (m t) -> p a t m", t=PACK),
+        )
+
+        v_words = [sb("v_words%d" % a, [P, S], U32) for a in range(PASSES)]
+        v_planes = [sb("v_planes%d" % a, [P, S], U8) for a in range(PASSES)]
+        c_words = sb("c_words", [P, S2], U32)
+        c_plane = sb("c_plane", [P, S2], U8)
+        w1_bf = [sb("w1_bf%d" % a, [P, PACK * H], BF16) for a in range(PASSES)]
+        w1_codes = [sb("w1_codes%d" % a, [P, H], U32) for a in range(PASSES)]
+        w1_planes = [sb("w1_planes%d" % a, [P, H], U8) for a in range(PASSES)]
+
+        def half_cols(half):
+            return slice(BANK * half, BANK * (half + 1))
+
+        def half_list(half):
+            return tokens[:, (BANK // 16) * half : (BANK // 16) * (half + 1)]
+
+        def gather_scales(a, half):
+            nc.vector.tensor_copy(out=v_planes[a][:, half_cols(half)], in_=v_scale_tab[:].bitcast(U8)[:, a, :].indirect(half_list(half)))
+
+        def gather_words(a, half):
+            nc.vector.tensor_copy(out=v_words[a][:, half_cols(half)], in_=v_word_tab[a][:].bitcast(U32).indirect(half_list(half)))
+
+        def round_w1(a):
+            nc.scalar.copy(
+                out=w1_bf[a][:].rearrange("p (t m j) -> p m t j", t=PACK, j=PACK),
+                in_=w1_raw[a][:].rearrange("p j (m t) -> p m t j", t=PACK),
+            )
+
+        def quantize_w1(a):
+            nc.vector.quantize_mx(out=w1_codes[a][:].bitcast(FP8X4), scales=w1_planes[a][:], in_=w1_bf[a][:])
+
+        temp_ps = bank("temp_ps", 7)
+        nc.tensor.transpose(temp_ps[:, 0:P], temp_rows[:], ident[:])
+        neg_temp = sb("neg_temp", [P, TILES], F32)
+        nc.scalar.activation(out=neg_temp[:], in_=temp_ps[:, 0:TILES], func=ACT.Copy, scale=-1.0)
+
+        h_ps = [[bank("h_ps%d_%d" % (half, t), PACK * half + t) for t in range(PACK)] for half in range(HALVES)]
+
+        def pass_w4(a, half, t):
+            nc.tensor.matmul_mx(
+                out=h_ps[half][t][:],
+                lhsT=w4_codes[:, a, 2 * P * t : 2 * P * (t + 1)].bitcast(FP4X4),
+                lhsT_scale=w4_planes[:, a, P * t : P * (t + 1)],
+                rhs=v_words[a][:, half_cols(half)].bitcast(FP8X4),
+                rhs_scale=v_planes[a][:, half_cols(half)],
+                start=(a == 0),
+                stop=False,
+            )
+
+        def pass_w1(a, half, t):
+            nc.tensor.matmul_mx(
+                out=h_ps[half][t][:],
+                lhsT=w1_codes[a][:, P * t : P * (t + 1)].bitcast(FP8X4),
+                lhsT_scale=w1_planes[a][:, P * t : P * (t + 1)],
+                rhs=v_words[a][:, half_cols(half)].bitcast(FP8X4),
+                rhs_scale=v_planes[a][:, half_cols(half)],
+                start=False,
+                stop=(a == PASSES - 1),
+            )
+
+        round_w1(0)
+        round_w1(1)
+        for half in range(HALVES):
+            gather_scales(0, half)
+        for half in range(HALVES):
+            gather_words(0, half)
+            for t in range(PACK):
+                pass_w4(0, half, t)
+        quantize_w1(0)
+        for half in range(HALVES):
+            for t in range(PACK):
+                pass_w1(0, half, t)
+        gather_scales(1, 0)
+        quantize_w1(1)
+
+        h_planes = [sb("h_planes%d" % half, [P, PACK, BANK], BF16) for half in range(HALVES)]
+        for half in range(HALVES):
+            if half > 0:
+                gather_scales(1, half)
+            gather_words(1, half)
+            for t in range(PACK):
+                pass_w4(1, half, t)
+                pass_w1(1, half, t)
+                if (half, t) in VECTOR_PLANES:
+                    nc.vector.tensor_scalar(out=h_planes[half][:, t, :], in0=h_ps[half][t][:], scalar1=bias[:, t : t + 1], scalar2=None, op0=ALU.add)
+                else:
+                    nc.scalar.activation(out=h_planes[half][:, t, :], in_=h_ps[half][t][:], func=ACT.Identity, bias=bias[:, t : t + 1])
+
+        nc.vector.tensor_copy(out=c_plane[:], in_=c_scale_tab[:].bitcast(U8).indirect(experts[:]))
+        nc.vector.tensor_copy(out=c_words[:], in_=c_word_tab[:].bitcast(U32).indirect(experts[:]))
+
+        z_ps = []
+        sig = []
+        for pair in range(S // PAIR):
+            half, first = divmod(PAIR * pair, BANK)
+            h_bf = sb("h_bf%d" % pair, [P, PAIR, PACK], BF16)
+            nc.vector.tensor_copy(
+                out=h_bf[:].rearrange("p (c i) t -> p c t i", i=4),
+                in_=h_planes[half][:, :, first : first + PAIR].rearrange("p t (c i) -> p c t i", i=4),
+            )
+            h_codes = sb("h_codes%d" % pair, [P, PAIR], U32)
+            h_plane = sb("h_plane%d" % pair, [P, PAIR], U8)
+            nc.vector.quantize_mx(out=h_codes[:].bitcast(FP8X4), scales=h_plane[:], in_=h_bf[:].rearrange("p n t -> p (n t)"))
+            for sub in range(PAIR // P):
+                i = (PAIR // P) * pair + sub
+                z = bank("z_ps%d" % i, i)
+                nc.tensor.matmul_mx(
+                    out=z[:],
+                    lhsT=h_codes[:, P * sub : P * (sub + 1)].bitcast(FP8X4),
+                    lhsT_scale=h_plane[:, P * sub : P * (sub + 1)],
+                    rhs=c_words[:].bitcast(FP8X4),
+                    rhs_scale=c_plane[:],
+                    start=True,
+                    stop=True,
+                )
+                s = sb("sig%d" % i, [P, S2], F32)
+                nc.scalar.activation(out=s[:], in_=z[:], func=ACT.Sigmoid, scale=neg_temp[:, i : i + 1])
+                z_ps.append(z)
+                sig.append(s)
+
+        ln_floor = sb("ln_floor", [P, 1], F32)
+        nc.scalar.activation(out=ln_floor[:], in_=sig[TILES - 1][:, 0:1], func=ACT.Copy, scale=0.0, bias=LN_FLOOR)
+
+        neg_soft = []
+        for i in range(TILES):
+            ln = sb("ln%d" % i, [P, S2], F32)
+            nc.scalar.activation(out=ln[:], in_=sig[i][:], func=ACT.Ln, bias=ln_floor[:])
+            lc = sb("lc%d" % i, [P, S2], F32)
+            nc.vector.tensor_scalar(out=lc[:], in0=ln[:], scalar1=-SQRT_FLOOR, scalar2=None, op0=ALU.min)
+            u = sb("neg_soft%d" % i, [P, S2], F32)
+            nc.vector.scalar_tensor_tensor(out=u[:], in0=z_ps[i][:], scalar=neg_temp[:, i : i + 1], in1=lc[:], op0=ALU.mult, op1=ALU.min)
+            neg_soft.append(u)
+
+        for half in range(HALVES):
+            o_ps = [bank("o_ps%d_%d" % (half, q), PACK * half + q) for q in range(S2 // P)]
+            for q in range(S2 // P):
+                for sub in range(BANK // P):
+                    nc.tensor.transpose(o_ps[q][:, P * sub : P * (sub + 1)], neg_soft[(BANK // P) * half + sub][:, P * q : P * (q + 1)], ident[:])
+                res = sb("res%d_%d" % (half, q), [P, BANK], F32)
+                nc.scalar.activation(out=res[:], in_=o_ps[q][:], func=ACT.Sqrt, scale=-1.0)
+                nc.sync.dma_start(out=out[P * q : P * (q + 1), half_cols(half)], in_=res[:])

@@ -26,7 +26,7 @@ TILES = S // P
 PAIR = 2 * P
 LN_FLOOR = 2.0**-60
 SQRT_FLOOR = 2.0**-100
-VECTOR_PLANES = []
+VECTOR_PLANES = [(0, 2), (1, 2)]
 
 
 def tile_list_expert_routing_affinities_kernel(
@@ -46,10 +46,11 @@ def tile_list_expert_routing_affinities_kernel(
 
         tokens = lists.tile([P, S // 16], U16, name="tokens")
         experts = lists.tile([P, S2 // 16], U16, name="experts")
-        v_scale_tab = sb("v_scale_tab", [P, PASSES, T // 4], I32)
+        v_scale_tab = [sb("v_scale_tab%d" % a, [P, T // 4], I32) for a in range(2)]
         w4_scale_raw = sb("w4_scale_raw", [P, PASSES, H // 4], I32)
         c_scale_tab = sb("c_scale_tab", [P, T2 // 4], I32)
-        temp_rows = sb("temp_rows", [P, P], F32)
+        temps = sb("temps", [P, TILES], F32)
+        neg_temp = sb("neg_temp", [P, TILES], F32)
         bias = sb("bias", [P, PACK], F32)
         w4_raw = sb("w4_raw", [P, PASSES, H // 2], I32)
         w1_raw = [sb("w1_raw%d" % a, [P, PACK, H], F32) for a in range(PASSES)]
@@ -57,49 +58,8 @@ def tile_list_expert_routing_affinities_kernel(
         c_word_tab = sb("c_word_tab", [P, T2], I32)
         ident = sb("ident", [P, P], F32)
         warm = sb("warm", [P, 2], F32)
-
-        nc.vector.memset(v_scale_tab[:], 0)
-        nc.vector.memset(w4_scale_raw[:], 0)
-        nc.gpsimd.memset(temp_rows[:], 0.0)
-        nc.gpsimd.dma_start(out=temp_rows[0:TILES, :], in_=temp.rearrange("(i p) -> i p", p=P))
-        nc.gpsimd.dma_start(out=bias[:], in_=b1.rearrange("(p t) -> p t", t=PACK))
-        make_identity(nc, ident[:])
-        nc.gpsimd.memset(c_scale_tab[:], 0)
-        nc.scalar.activation(out=warm[:, 0:1], in_=ident[:, 0:1], func=ACT.Sigmoid)
-
-        def load_scale_rows(engine, plane, rows_of):
-            for quad in range(4):
-                engine.dma_start(out=plane(slice(32 * quad, 32 * quad + 4)), in_=rows_of(slice(4 * quad, 4 * quad + 4)).bitcast(I32))
-
-        def load_w1(a):
-            nc.sync.dma_start(out=w1_raw[a][:], in_=w1[512 * a : 512 * (a + 1), :].rearrange("(p j) c -> p j c", j=PACK))
-
-        def load_v(a):
-            nc.sync.dma_start(out=v_word_tab[a][:], in_=tab_words[a].rearrange("p t i -> p (t i)").bitcast(I32))
-
-        nc.sync.dma_start(tokens[:], offs)
-        nc.sync.dma_start(out=w4_raw[:], in_=w4_words.rearrange("a p n -> p a n").bitcast(I32))
-        load_scale_rows(nc.sync, lambda live: v_scale_tab[live, :, :], lambda rows: tab_scales[:, rows, :].rearrange("a r n -> r a n"))
-        load_w1(0)
-        load_v(0)
-        load_scale_rows(nc.sync, lambda live: w4_scale_raw[live, :, :], lambda rows: w4_scales[:, rows, :].rearrange("a r n -> r a n"))
-        load_w1(1)
-        load_v(1)
-        nc.sync.dma_start(experts[:], offs2)
-        nc.sync.dma_start(out=c_word_tab[:], in_=tab2_words[0].rearrange("p t i -> p (t i)").bitcast(I32))
-        load_scale_rows(nc.gpsimd, lambda live: c_scale_tab[live, :], lambda rows: tab2_scales[0, rows, :])
-
         w4_codes = sb("w4_codes", [P, PASSES, 2 * H], U8)
         w4_planes = sb("w4_planes", [P, PASSES, H], U8)
-        nc.vector.tensor_copy(
-            out=w4_planes[:].rearrange("p a (t m) -> p a t m", t=PACK),
-            in_=w4_scale_raw[:].bitcast(U8).rearrange("p a (m t) -> p a t m", t=PACK),
-        )
-        nc.vector.tensor_copy(
-            out=w4_codes[:].bitcast(U16).rearrange("p a (t m) -> p a t m", t=PACK),
-            in_=w4_raw[:].bitcast(U16).rearrange("p a (m t) -> p a t m", t=PACK),
-        )
-
         v_words = [sb("v_words%d" % a, [P, S], U32) for a in range(PASSES)]
         v_planes = [sb("v_planes%d" % a, [P, S], U8) for a in range(PASSES)]
         c_words = sb("c_words", [P, S2], U32)
@@ -107,6 +67,10 @@ def tile_list_expert_routing_affinities_kernel(
         w1_bf = [sb("w1_bf%d" % a, [P, PACK * H], BF16) for a in range(PASSES)]
         w1_codes = [sb("w1_codes%d" % a, [P, H], U32) for a in range(PASSES)]
         w1_planes = [sb("w1_planes%d" % a, [P, H], U8) for a in range(PASSES)]
+        h_planes = [sb("h_planes%d" % half, [P, PACK, BANK], BF16) for half in range(HALVES)]
+        h_ps = [[bank("h_ps%d_%d" % (half, t), PACK * half + t) for t in range(PACK)] for half in range(HALVES)]
+        z_ps = []
+        sig = []
 
         def half_cols(half):
             return slice(BANK * half, BANK * (half + 1))
@@ -114,27 +78,30 @@ def tile_list_expert_routing_affinities_kernel(
         def half_list(half):
             return tokens[:, (BANK // 16) * half : (BANK // 16) * (half + 1)]
 
+        def load_scale_rows(engine, plane, rows_of):
+            for quad in range(4):
+                engine.dma_start(out=plane(slice(32 * quad, 32 * quad + 4)), in_=rows_of(slice(4 * quad, 4 * quad + 4)).bitcast(I32))
+
+        def load_w1(engine, a, c0, c1):
+            engine.dma_start(out=w1_raw[a][:, :, c0:c1], in_=w1[512 * a : 512 * (a + 1), c0:c1].rearrange("(p j) c -> p j c", j=PACK))
+
+        def load_v(engine, a):
+            engine.dma_start(out=v_word_tab[a][:], in_=tab_words[a].rearrange("p t i -> p (t i)").bitcast(I32))
+
         def gather_scales(a, half):
-            nc.vector.tensor_copy(out=v_planes[a][:, half_cols(half)], in_=v_scale_tab[:].bitcast(U8)[:, a, :].indirect(half_list(half)))
+            nc.vector.tensor_copy(out=v_planes[a][:, half_cols(half)], in_=v_scale_tab[a][:].bitcast(U8).indirect(half_list(half)))
 
         def gather_words(a, half):
             nc.vector.tensor_copy(out=v_words[a][:, half_cols(half)], in_=v_word_tab[a][:].bitcast(U32).indirect(half_list(half)))
 
-        def round_w1(a):
+        def round_w1(a, c0, c1):
             nc.scalar.copy(
-                out=w1_bf[a][:].rearrange("p (t m j) -> p m t j", t=PACK, j=PACK),
-                in_=w1_raw[a][:].rearrange("p j (m t) -> p m t j", t=PACK),
+                out=w1_bf[a][:].rearrange("p (t m j) -> p m t j", t=PACK, j=PACK)[:, c0 // PACK : c1 // PACK, :, :],
+                in_=w1_raw[a][:, :, c0:c1].rearrange("p j (m t) -> p m t j", t=PACK),
             )
 
         def quantize_w1(a):
             nc.vector.quantize_mx(out=w1_codes[a][:].bitcast(FP8X4), scales=w1_planes[a][:], in_=w1_bf[a][:])
-
-        temp_ps = bank("temp_ps", 7)
-        nc.tensor.transpose(temp_ps[:, 0:P], temp_rows[:], ident[:])
-        neg_temp = sb("neg_temp", [P, TILES], F32)
-        nc.scalar.activation(out=neg_temp[:], in_=temp_ps[:, 0:TILES], func=ACT.Copy, scale=-1.0)
-
-        h_ps = [[bank("h_ps%d_%d" % (half, t), PACK * half + t) for t in range(PACK)] for half in range(HALVES)]
 
         def pass_w4(a, half, t):
             nc.tensor.matmul_mx(
@@ -158,40 +125,20 @@ def tile_list_expert_routing_affinities_kernel(
                 stop=(a == PASSES - 1),
             )
 
-        round_w1(0)
-        round_w1(1)
-        for half in range(HALVES):
-            gather_scales(0, half)
-        for half in range(HALVES):
-            gather_words(0, half)
-            for t in range(PACK):
-                pass_w4(0, half, t)
-        quantize_w1(0)
-        for half in range(HALVES):
-            for t in range(PACK):
-                pass_w1(0, half, t)
-        gather_scales(1, 0)
-        quantize_w1(1)
+        def leave_bank(half, t):
+            if (half, t) in VECTOR_PLANES:
+                nc.vector.tensor_scalar(out=h_planes[half][:, t, :], in0=h_ps[half][t][:], scalar1=bias[:, t : t + 1], scalar2=None, op0=ALU.add)
+            else:
+                nc.scalar.activation(out=h_planes[half][:, t, :], in_=h_ps[half][t][:], func=ACT.Identity, bias=bias[:, t : t + 1])
 
-        h_planes = [sb("h_planes%d" % half, [P, PACK, BANK], BF16) for half in range(HALVES)]
-        for half in range(HALVES):
-            if half > 0:
-                gather_scales(1, half)
-            gather_words(1, half)
+        def finish_half(half, with_w4):
             for t in range(PACK):
-                pass_w4(1, half, t)
+                if with_w4:
+                    pass_w4(1, half, t)
                 pass_w1(1, half, t)
-                if (half, t) in VECTOR_PLANES:
-                    nc.vector.tensor_scalar(out=h_planes[half][:, t, :], in0=h_ps[half][t][:], scalar1=bias[:, t : t + 1], scalar2=None, op0=ALU.add)
-                else:
-                    nc.scalar.activation(out=h_planes[half][:, t, :], in_=h_ps[half][t][:], func=ACT.Identity, bias=bias[:, t : t + 1])
+                leave_bank(half, t)
 
-        nc.vector.tensor_copy(out=c_plane[:], in_=c_scale_tab[:].bitcast(U8).indirect(experts[:]))
-        nc.vector.tensor_copy(out=c_words[:], in_=c_word_tab[:].bitcast(U32).indirect(experts[:]))
-
-        z_ps = []
-        sig = []
-        for pair in range(S // PAIR):
+        def score_pair(pair):
             half, first = divmod(PAIR * pair, BANK)
             h_bf = sb("h_bf%d" % pair, [P, PAIR, PACK], BF16)
             nc.vector.tensor_copy(
@@ -218,8 +165,70 @@ def tile_list_expert_routing_affinities_kernel(
                 z_ps.append(z)
                 sig.append(s)
 
+        nc.vector.memset(v_scale_tab[0][:], 0)
+        nc.sync.dma_start(out=w4_raw[:], in_=w4_words.rearrange("a p n -> p a n").bitcast(I32))
+        nc.sync.dma_start(tokens[:], offs)
+        nc.gpsimd.memset(warm[:], 0.0)
+        nc.gpsimd.memset(w4_scale_raw[:], 0)
+        nc.sync.dma_start(experts[:], offs2)
+        load_scale_rows(nc.sync, lambda live: v_scale_tab[0][live, :], lambda rows: tab_scales[0, rows, :])
+        load_v(nc.sync, 0)
+        load_scale_rows(nc.sync, lambda live: w4_scale_raw[live, :, :], lambda rows: w4_scales[:, rows, :].rearrange("a r n -> r a n"))
+        load_w1(nc.sync, 0, 0, H)
+        nc.vector.memset(v_scale_tab[1][:], 0)
+        nc.vector.tensor_copy(
+            out=w4_codes[:].bitcast(U16).rearrange("p a (t m) -> p a t m", t=PACK),
+            in_=w4_raw[:].bitcast(U16).rearrange("p a (m t) -> p a t m", t=PACK),
+        )
+        nc.sync.dma_start(out=c_word_tab[:], in_=tab2_words[0].rearrange("p t i -> p (t i)").bitcast(I32))
+        load_w1(nc.sync, 1, H // 2, H)
+        nc.vector.tensor_copy(
+            out=w4_planes[:].rearrange("p a (t m) -> p a t m", t=PACK),
+            in_=w4_scale_raw[:].bitcast(U8).rearrange("p a (m t) -> p a t m", t=PACK),
+        )
+        gather_words(0, 1)
+        nc.sync.dma_start(out=bias[:], in_=b1.rearrange("(p t) -> p t", t=PACK))
+        round_w1(0, 0, H)
+        gather_scales(0, 1)
+        gather_scales(0, 0)
+        load_scale_rows(nc.sync, lambda live: v_scale_tab[1][live, :], lambda rows: tab_scales[1, rows, :])
+        nc.gpsimd.memset(c_scale_tab[:], 0)
+        for t in range(PACK):
+            pass_w4(0, 1, t)
+        gather_scales(1, 1)
+        load_w1(nc.sync, 1, 0, H // 2)
+        quantize_w1(0)
+        load_v(nc.sync, 1)
+        for t in range(PACK):
+            pass_w1(0, 1, t)
+        load_scale_rows(nc.sync, lambda live: c_scale_tab[live, :], lambda rows: tab2_scales[0, rows, :])
+        nc.scalar.activation(out=warm[:, 1:2], in_=warm[:, 0:1], func=ACT.Sigmoid)
+        gather_words(0, 0)
+        with nc.allow_non_contiguous_dma(reason="one token's temperature to a partition"):
+            nc.sync.dma_start(out=temps[:], in_=temp.rearrange("(i p) -> p i", p=P))
+        for t in range(PACK):
+            pass_w4(0, 0, t)
+        for t in range(PACK):
+            pass_w1(0, 0, t)
+        round_w1(1, 0, H // 2)
+        round_w1(1, H // 2, H)
+        make_identity(nc, ident[:])
+        quantize_w1(1)
+        nc.gpsimd.tensor_scalar(out=neg_temp[:], in0=temps[:], scalar1=-1.0, scalar2=0.0, op0=ALU.mult, op1=ALU.add)
+        nc.vector.tensor_copy(out=c_plane[:], in_=c_scale_tab[:].bitcast(U8).indirect(experts[:]))
+        gather_words(1, 0)
+        nc.vector.tensor_copy(out=c_words[:], in_=c_word_tab[:].bitcast(U32).indirect(experts[:]))
+        gather_scales(1, 0)
+        finish_half(0, True)
+        score_pair(0)
+        gather_words(1, 1)
+        finish_half(1, True)
+        score_pair(1)
+        score_pair(2)
+        score_pair(3)
+
         ln_floor = sb("ln_floor", [P, 1], F32)
-        nc.scalar.activation(out=ln_floor[:], in_=sig[TILES - 1][:, 0:1], func=ACT.Copy, scale=0.0, bias=LN_FLOOR)
+        nc.gpsimd.tensor_scalar(out=ln_floor[:], in0=sig[TILES - 2][:, 0:1], scalar1=0.0, scalar2=LN_FLOOR, op0=ALU.mult, op1=ALU.add)
 
         neg_soft = []
         for i in range(TILES):
@@ -231,11 +240,18 @@ def tile_list_expert_routing_affinities_kernel(
             nc.vector.scalar_tensor_tensor(out=u[:], in0=z_ps[i][:], scalar=neg_temp[:, i : i + 1], in1=lc[:], op0=ALU.mult, op1=ALU.min)
             neg_soft.append(u)
 
-        for half in range(HALVES):
-            o_ps = [bank("o_ps%d_%d" % (half, q), PACK * half + q) for q in range(S2 // P)]
-            for q in range(S2 // P):
-                for sub in range(BANK // P):
-                    nc.tensor.transpose(o_ps[q][:, P * sub : P * (sub + 1)], neg_soft[(BANK // P) * half + sub][:, P * q : P * (q + 1)], ident[:])
-                res = sb("res%d_%d" % (half, q), [P, BANK], F32)
-                nc.scalar.activation(out=res[:], in_=o_ps[q][:], func=ACT.Sqrt, scale=-1.0)
-                nc.sync.dma_start(out=out[P * q : P * (q + 1), half_cols(half)], in_=res[:])
+        for pair in range(S // PAIR):
+            for b in range(2):
+                o_ps = bank("o_ps%d_%d" % (pair, b), 2 * pair + b)
+                for sub in range(2):
+                    for q in range(2):
+                        nc.tensor.transpose(
+                            o_ps[:, PAIR * q + P * sub : PAIR * q + P * (sub + 1)],
+                            neg_soft[2 * pair + sub][:, P * (2 * b + q) : P * (2 * b + q + 1)],
+                            ident[:],
+                        )
+                res = sb("res%d_%d" % (pair, b), [P, 2, PAIR], F32)
+                nc.scalar.activation(out=res[:].rearrange("p q j -> p (q j)"), in_=o_ps[:], func=ACT.Sqrt, scale=-1.0)
+                nc.sync.dma_start(
+                    out=out[PAIR * b : PAIR * (b + 1), PAIR * pair : PAIR * (pair + 1)].rearrange("(q p) j -> p q j", p=P), in_=res[:]
+                )

@@ -26,7 +26,7 @@ TILES = S // P
 PAIR = 2 * P
 LN_FLOOR = 2.0**-60
 SQRT_FLOOR = 2.0**-100
-VECTOR_PLANES = [(0, 2), (1, 2)]
+VECTOR_PLANES = []
 
 
 def tile_list_expert_routing_affinities_kernel(
@@ -46,10 +46,9 @@ def tile_list_expert_routing_affinities_kernel(
 
         tokens = lists.tile([P, S // 16], U16, name="tokens")
         experts = lists.tile([P, S2 // 16], U16, name="experts")
-        v_scale_tab = [sb("v_scale_tab%d" % a, [P, T // 4], I32) for a in range(2)]
+        v_scale_tab = [sb("v_scale_tab%d" % a, [P, T // 4], I32) for a in range(1)]
         w4_scale_raw = sb("w4_scale_raw", [P, PASSES, H // 4], I32)
         c_scale_tab = sb("c_scale_tab", [P, T2 // 4], I32)
-        temps = sb("temps", [P, TILES], F32)
         neg_temp = sb("neg_temp", [P, TILES], F32)
         bias = sb("bias", [P, PACK], F32)
         w4_raw = sb("w4_raw", [P, PASSES, H // 2], I32)
@@ -61,14 +60,17 @@ def tile_list_expert_routing_affinities_kernel(
         w4_codes = sb("w4_codes", [P, PASSES, 2 * H], U8)
         w4_planes = sb("w4_planes", [P, PASSES, H], U8)
         v_words = [sb("v_words%d" % a, [P, S], U32) for a in range(PASSES)]
-        v_planes = [sb("v_planes%d" % a, [P, S], U8) for a in range(PASSES)]
+        v_scales = sb("v_scales", [P, S], U8)
+        v_plane_pair = sb("v_plane_pair", [P, PASSES, S], U8)
+        v_planes = [v_plane_pair[:, a, :] for a in range(PASSES)]
+        temp_rows = sb("temp_rows", [P, P], F32)
         c_words = sb("c_words", [P, S2], U32)
         c_plane = sb("c_plane", [P, S2], U8)
         w1_bf = [sb("w1_bf%d" % a, [P, PACK * H], BF16) for a in range(PASSES)]
         w1_codes = [sb("w1_codes%d" % a, [P, H], U32) for a in range(PASSES)]
         w1_planes = [sb("w1_planes%d" % a, [P, H], U8) for a in range(PASSES)]
         h_planes = [sb("h_planes%d" % half, [P, PACK, BANK], BF16) for half in range(HALVES)]
-        h_ps = [[bank("h_ps%d_%d" % (half, t), PACK * half + t) for t in range(PACK)] for half in range(HALVES)]
+        h_ps = [[bank("h_ps0_%d" % t, t) for t in range(PACK)]]
         z_ps = []
         sig = []
 
@@ -89,13 +91,20 @@ def tile_list_expert_routing_affinities_kernel(
             engine.dma_start(out=v_word_tab[a][:], in_=tab_words[a].rearrange("p t i -> p (t i)").bitcast(I32))
 
         def gather_scales(a, half):
-            nc.vector.tensor_copy(out=v_planes[a][:, half_cols(half)], in_=v_scale_tab[a][:].bitcast(U8).indirect(half_list(half)))
+            nc.vector.tensor_copy(out=v_scales[:, half_cols(half)], in_=v_scale_tab[a][:].bitcast(U8).indirect(half_list(half)))
 
         def gather_words(a, half):
             nc.vector.tensor_copy(out=v_words[a][:, half_cols(half)], in_=v_word_tab[a][:].bitcast(U32).indirect(half_list(half)))
 
-        def round_w1(a, c0, c1):
-            nc.scalar.copy(
+        def move_scale_rows(engine, a, cols):
+            for quad in range(4):
+                first = 16 * a + 4 * quad
+                engine.dma_start(
+                    out=v_planes[a][32 * quad : 32 * quad + 4, cols].bitcast(I32), in_=v_scales[first : first + 4, cols].bitcast(I32)
+                )
+
+        def round_w1(copy, a, c0, c1):
+            copy(
                 out=w1_bf[a][:].rearrange("p (t m j) -> p m t j", t=PACK, j=PACK)[:, c0 // PACK : c1 // PACK, :, :],
                 in_=w1_raw[a][:, :, c0:c1].rearrange("p j (m t) -> p m t j", t=PACK),
             )
@@ -138,18 +147,18 @@ def tile_list_expert_routing_affinities_kernel(
                 pass_w1(1, half, t)
                 leave_bank(half, t)
 
-        def score_pair(pair):
-            half, first = divmod(PAIR * pair, BANK)
-            h_bf = sb("h_bf%d" % pair, [P, PAIR, PACK], BF16)
+        def score(first_token, width):
+            half, first = divmod(first_token, BANK)
+            h_bf = sb("h_bf%d" % first_token, [P, width, PACK], BF16)
             nc.vector.tensor_copy(
                 out=h_bf[:].rearrange("p (c i) t -> p c t i", i=4),
-                in_=h_planes[half][:, :, first : first + PAIR].rearrange("p t (c i) -> p c t i", i=4),
+                in_=h_planes[half][:, :, first : first + width].rearrange("p t (c i) -> p c t i", i=4),
             )
-            h_codes = sb("h_codes%d" % pair, [P, PAIR], U32)
-            h_plane = sb("h_plane%d" % pair, [P, PAIR], U8)
+            h_codes = sb("h_codes%d" % first_token, [P, width], U32)
+            h_plane = sb("h_plane%d" % first_token, [P, width], U8)
             nc.vector.quantize_mx(out=h_codes[:].bitcast(FP8X4), scales=h_plane[:], in_=h_bf[:].rearrange("p n t -> p (n t)"))
-            for sub in range(PAIR // P):
-                i = (PAIR // P) * pair + sub
+            for sub in range(width // P):
+                i = first_token // P + sub
                 z = bank("z_ps%d" % i, i)
                 nc.tensor.matmul_mx(
                     out=z[:],
@@ -165,67 +174,71 @@ def tile_list_expert_routing_affinities_kernel(
                 z_ps.append(z)
                 sig.append(s)
 
-        nc.vector.memset(v_scale_tab[0][:], 0)
-        nc.sync.dma_start(out=w4_raw[:], in_=w4_words.rearrange("a p n -> p a n").bitcast(I32))
-        nc.sync.dma_start(tokens[:], offs)
-        nc.gpsimd.memset(warm[:], 0.0)
         nc.gpsimd.memset(w4_scale_raw[:], 0)
-        nc.sync.dma_start(experts[:], offs2)
-        load_scale_rows(nc.sync, lambda live: v_scale_tab[0][live, :], lambda rows: tab_scales[0, rows, :])
-        load_v(nc.sync, 0)
         load_scale_rows(nc.sync, lambda live: w4_scale_raw[live, :, :], lambda rows: w4_scales[:, rows, :].rearrange("a r n -> r a n"))
+        nc.scalar.dma_start(out=v_scale_tab[0][0:32, :], in_=tab_scales.rearrange("a q t -> (a q) t").bitcast(I32))
+        nc.sync.dma_start(tokens[:], offs)
+        nc.vector.memset(v_scale_tab[0][32:64, :], 0)
+        nc.vector.memset(v_scale_tab[0][64:128, :], 0)
+        nc.gpsimd.memset(v_plane_pair[:].bitcast(I32), 0)
+        load_v(nc.scalar, 0)
+        nc.vector.tensor_copy(out=v_scales[:], in_=v_scale_tab[0][:].bitcast(U8).indirect(tokens[:]))
         load_w1(nc.sync, 0, 0, H)
-        nc.vector.memset(v_scale_tab[1][:], 0)
-        nc.vector.tensor_copy(
-            out=w4_codes[:].bitcast(U16).rearrange("p a (t m) -> p a t m", t=PACK),
-            in_=w4_raw[:].bitcast(U16).rearrange("p a (m t) -> p a t m", t=PACK),
-        )
-        nc.sync.dma_start(out=c_word_tab[:], in_=tab2_words[0].rearrange("p t i -> p (t i)").bitcast(I32))
-        load_w1(nc.sync, 1, H // 2, H)
         nc.vector.tensor_copy(
             out=w4_planes[:].rearrange("p a (t m) -> p a t m", t=PACK),
             in_=w4_scale_raw[:].bitcast(U8).rearrange("p a (m t) -> p a t m", t=PACK),
         )
-        gather_words(0, 1)
-        nc.sync.dma_start(out=bias[:], in_=b1.rearrange("(p t) -> p t", t=PACK))
-        round_w1(0, 0, H)
-        gather_scales(0, 1)
-        gather_scales(0, 0)
-        load_scale_rows(nc.sync, lambda live: v_scale_tab[1][live, :], lambda rows: tab_scales[1, rows, :])
-        nc.gpsimd.memset(c_scale_tab[:], 0)
-        for t in range(PACK):
-            pass_w4(0, 1, t)
-        gather_scales(1, 1)
+        nc.gpsimd.memset(temp_rows[:], 0.0)
+        nc.scalar.dma_start(out=w4_raw[:], in_=w4_words.rearrange("a p n -> p a n").bitcast(I32))
+        nc.sync.dma_start(out=temp_rows[0:TILES, :], in_=temp.rearrange("(i p) -> i p", p=P))
+        make_identity(nc, ident[:])
+        move_scale_rows(nc.sync, 0, slice(0, S))
         load_w1(nc.sync, 1, 0, H // 2)
-        quantize_w1(0)
+        load_w1(nc.sync, 1, H // 2, H)
+        round_w1(nc.scalar.copy, 1, 0, H // 2)
+        round_w1(nc.vector.tensor_copy, 1, H // 2, H)
         load_v(nc.sync, 1)
-        for t in range(PACK):
-            pass_w1(0, 1, t)
-        load_scale_rows(nc.sync, lambda live: c_scale_tab[live, :], lambda rows: tab2_scales[0, rows, :])
-        nc.scalar.activation(out=warm[:, 1:2], in_=warm[:, 0:1], func=ACT.Sigmoid)
+        move_scale_rows(nc.sync, 1, slice(0, S))
+        nc.gpsimd.memset(warm[:], 0.0)
+        nc.vector.tensor_copy(
+            out=w4_codes[:].bitcast(U16).rearrange("p a (t m) -> p a t m", t=PACK),
+            in_=w4_raw[:].bitcast(U16).rearrange("p a (m t) -> p a t m", t=PACK),
+        )
         gather_words(0, 0)
-        with nc.allow_non_contiguous_dma(reason="one token's temperature to a partition"):
-            nc.sync.dma_start(out=temps[:], in_=temp.rearrange("(i p) -> p i", p=P))
+        round_w1(nc.scalar.copy, 0, 0, H)
+        gather_words(0, 1)
+        nc.sync.dma_start(experts[:], offs2)
         for t in range(PACK):
             pass_w4(0, 0, t)
+        quantize_w1(0)
+        gather_words(1, 0)
+        temp_ps = bank("temp_ps", 7)
+        nc.tensor.transpose(temp_ps[:, 0:P], temp_rows[:], ident[:])
+        nc.scalar.activation(out=neg_temp[:], in_=temp_ps[:, 0:TILES], func=ACT.Copy, scale=-1.0)
+        h_ps.append([bank("h_ps1_%d" % t, PACK + t) for t in range(PACK)])
+        gather_words(1, 1)
+        nc.sync.dma_start(out=c_word_tab[:], in_=tab2_words[0].rearrange("p t i -> p (t i)").bitcast(I32))
+        nc.vector.tensor_copy(out=c_words[:], in_=c_word_tab[:].bitcast(U32).indirect(experts[:]))
+        for t in range(PACK):
+            pass_w4(0, 1, t)
+        nc.gpsimd.memset(c_scale_tab[:], 0)
+        for t in range(PACK):
+            pass_w1(0, 1, t)
+        quantize_w1(1)
+        load_scale_rows(nc.sync, lambda live: c_scale_tab[live, :], lambda rows: tab2_scales[0, rows, :])
+        nc.scalar.activation(out=warm[:, 1:2], in_=warm[:, 0:1], func=ACT.Sigmoid)
         for t in range(PACK):
             pass_w1(0, 0, t)
-        round_w1(1, 0, H // 2)
-        round_w1(1, H // 2, H)
-        make_identity(nc, ident[:])
-        quantize_w1(1)
-        nc.gpsimd.tensor_scalar(out=neg_temp[:], in0=temps[:], scalar1=-1.0, scalar2=0.0, op0=ALU.mult, op1=ALU.add)
+        nc.sync.dma_start(out=bias[:], in_=b1.rearrange("(p t) -> p t", t=PACK))
         nc.vector.tensor_copy(out=c_plane[:], in_=c_scale_tab[:].bitcast(U8).indirect(experts[:]))
-        gather_words(1, 0)
-        nc.vector.tensor_copy(out=c_words[:], in_=c_word_tab[:].bitcast(U32).indirect(experts[:]))
-        gather_scales(1, 0)
         finish_half(0, True)
-        score_pair(0)
-        gather_words(1, 1)
         finish_half(1, True)
-        score_pair(1)
-        score_pair(2)
-        score_pair(3)
+        score(PAIR * 0, P)
+        score(PAIR * 0 + P, P)
+        score(PAIR * 1, PAIR)
+        score(PAIR * 2, P)
+        score(PAIR * 2 + P, P)
+        score(PAIR * 3, PAIR)
 
         ln_floor = sb("ln_floor", [P, 1], F32)
         nc.gpsimd.tensor_scalar(out=ln_floor[:], in0=sig[TILES - 2][:, 0:1], scalar1=0.0, scalar2=LN_FLOOR, op0=ALU.mult, op1=ALU.add)

@@ -174,97 +174,94 @@ def tile_list_expert_routing_affinities_kernel(
                 z_ps.append(z)
                 sig.append(s)
 
-        nc.gpsimd.memset(w4_scale_raw[:], 0)
-        load_scale_rows(nc.sync, lambda live: w4_scale_raw[live, :, :], lambda rows: w4_scales[:, rows, :].rearrange("a r n -> r a n"))
-        nc.scalar.dma_start(out=v_scale_tab[0][0:32, :], in_=tab_scales.rearrange("a q t -> (a q) t").bitcast(I32))
-        nc.sync.dma_start(tokens[:], offs)
+        nc.gpsimd.memset(warm[:], 0.0)
+        nc.scalar.activation(out=warm[:, 1:2], in_=warm[:, 0:1], func=ACT.Sigmoid)
         nc.vector.memset(v_scale_tab[0][32:64, :], 0)
         nc.vector.memset(v_scale_tab[0][64:128, :], 0)
-        nc.gpsimd.memset(v_plane_pair[:].bitcast(I32), 0)
-        load_v(nc.scalar, 0)
-        nc.vector.tensor_copy(out=v_scales[:], in_=v_scale_tab[0][:].bitcast(U8).indirect(tokens[:]))
-        load_w1(nc.sync, 0, 0, H)
-        nc.vector.tensor_copy(
-            out=w4_planes[:].rearrange("p a (t m) -> p a t m", t=PACK),
-            in_=w4_scale_raw[:].bitcast(U8).rearrange("p a (m t) -> p a t m", t=PACK),
-        )
+        nc.gpsimd.memset(w4_scale_raw[:], 0)
         nc.gpsimd.memset(temp_rows[:], 0.0)
-        nc.scalar.dma_start(out=w4_raw[:], in_=w4_words.rearrange("a p n -> p a n").bitcast(I32))
-        nc.sync.dma_start(out=temp_rows[0:TILES, :], in_=temp.rearrange("(i p) -> i p", p=P))
+        nc.gpsimd.memset(v_plane_pair[:].bitcast(I32), 0)
+        nc.gpsimd.memset(c_scale_tab[:], 0)
         make_identity(nc, ident[:])
+        nc.sync.dma_start(out=v_scale_tab[0][0:32, :], in_=tab_scales.rearrange("a q t -> (a q) t").bitcast(I32))
+        nc.sync.dma_start(tokens[:], offs)
+        nc.sync.dma_start(out=w4_raw[:], in_=w4_words.rearrange("a p n -> p a n").bitcast(I32))
+        load_v(nc.sync, 0)
+        load_w1(nc.sync, 0, 0, H)
+        load_scale_rows(nc.scalar, lambda live: w4_scale_raw[live, :, :], lambda rows: w4_scales[:, rows, :].rearrange("a r n -> r a n"))
+        nc.scalar.dma_start(out=temp_rows[0:TILES, :], in_=temp.rearrange("(i p) -> i p", p=P))
+        nc.vector.tensor_copy(out=v_scales[:], in_=v_scale_tab[0][:].bitcast(U8).indirect(tokens[:]))
         move_scale_rows(nc.sync, 0, slice(0, S))
-        load_w1(nc.sync, 1, 0, H // 2)
-        load_w1(nc.sync, 1, H // 2, H)
-        round_w1(nc.scalar.copy, 1, 0, H // 2)
-        round_w1(nc.vector.tensor_copy, 1, H // 2, H)
+        load_w1(nc.sync, 1, 0, H)
         load_v(nc.sync, 1)
+        nc.sync.dma_start(out=bias[:], in_=b1.rearrange("(p t) -> p t", t=PACK))
+        nc.sync.dma_start(experts[:], offs2)
         move_scale_rows(nc.sync, 1, slice(0, S))
-        nc.gpsimd.memset(warm[:], 0.0)
+        load_scale_rows(nc.sync, lambda live: c_scale_tab[live, :], lambda rows: tab2_scales[0, rows, :])
+        nc.sync.dma_start(out=c_word_tab[:], in_=tab2_words[0].rearrange("p t i -> p (t i)").bitcast(I32))
         nc.vector.tensor_copy(
             out=w4_codes[:].bitcast(U16).rearrange("p a (t m) -> p a t m", t=PACK),
             in_=w4_raw[:].bitcast(U16).rearrange("p a (m t) -> p a t m", t=PACK),
         )
-        gather_words(0, 0)
-        round_w1(nc.scalar.copy, 0, 0, H)
-        gather_words(0, 1)
-        nc.sync.dma_start(experts[:], offs2)
-        for t in range(PACK):
-            pass_w4(0, 0, t)
-        quantize_w1(0)
-        gather_words(1, 0)
+        nc.vector.tensor_copy(
+            out=w4_planes[:].rearrange("p a (t m) -> p a t m", t=PACK),
+            in_=w4_scale_raw[:].bitcast(U8).rearrange("p a (m t) -> p a t m", t=PACK),
+        )
         temp_ps = bank("temp_ps", 7)
         nc.tensor.transpose(temp_ps[:, 0:P], temp_rows[:], ident[:])
         nc.scalar.activation(out=neg_temp[:], in_=temp_ps[:, 0:TILES], func=ACT.Copy, scale=-1.0)
         h_ps.append([bank("h_ps1_%d" % t, PACK + t) for t in range(PACK)])
-        gather_words(1, 1)
-        nc.sync.dma_start(out=c_word_tab[:], in_=tab2_words[0].rearrange("p t i -> p (t i)").bitcast(I32))
-        nc.vector.tensor_copy(out=c_words[:], in_=c_word_tab[:].bitcast(U32).indirect(experts[:]))
+        gather_words(0, 0)
+        for t in range(PACK):
+            pass_w4(0, 0, t)
+        gather_words(0, 1)
         for t in range(PACK):
             pass_w4(0, 1, t)
-        nc.gpsimd.memset(c_scale_tab[:], 0)
-        for t in range(PACK):
-            pass_w1(0, 1, t)
-        quantize_w1(1)
-        load_scale_rows(nc.sync, lambda live: c_scale_tab[live, :], lambda rows: tab2_scales[0, rows, :])
-        nc.scalar.activation(out=warm[:, 1:2], in_=warm[:, 0:1], func=ACT.Sigmoid)
+        round_w1(nc.scalar.copy, 0, 0, H // 2)
+        round_w1(nc.vector.tensor_copy, 0, H // 2, H)
+        quantize_w1(0)
         for t in range(PACK):
             pass_w1(0, 0, t)
-        nc.sync.dma_start(out=bias[:], in_=b1.rearrange("(p t) -> p t", t=PACK))
-        nc.vector.tensor_copy(out=c_plane[:], in_=c_scale_tab[:].bitcast(U8).indirect(experts[:]))
+        for t in range(PACK):
+            pass_w1(0, 1, t)
+        round_w1(nc.scalar.copy, 1, 0, H // 2)
+        round_w1(nc.vector.tensor_copy, 1, H // 2, H)
+        quantize_w1(1)
+        gather_words(1, 0)
         finish_half(0, True)
+        gather_words(1, 1)
         finish_half(1, True)
+        nc.vector.tensor_copy(out=c_plane[:], in_=c_scale_tab[:].bitcast(U8).indirect(experts[:]))
+        nc.vector.tensor_copy(out=c_words[:], in_=c_word_tab[:].bitcast(U32).indirect(experts[:]))
         score(PAIR * 0, P)
         score(PAIR * 0 + P, P)
         score(PAIR * 1, PAIR)
         score(PAIR * 2, P)
         score(PAIR * 2 + P, P)
-        score(PAIR * 3, PAIR)
+        score(PAIR * 3, P)
+        score(PAIR * 3 + P, P)
 
         ln_floor = sb("ln_floor", [P, 1], F32)
         nc.gpsimd.tensor_scalar(out=ln_floor[:], in0=sig[TILES - 2][:, 0:1], scalar1=0.0, scalar2=LN_FLOOR, op0=ALU.mult, op1=ALU.add)
 
-        neg_soft = []
+        neg_relu = []
         for i in range(TILES):
+            nz = sb("neg_relu%d" % i, [P, S2], F32)
+            nc.vector.tensor_scalar(out=nz[:], in0=z_ps[i][:], scalar1=neg_temp[:, i : i + 1], scalar2=-SQRT_FLOOR, op0=ALU.mult, op1=ALU.min)
+            neg_relu.append(nz)
+
+        o_ps = [bank("o_ps%d" % b, b) for b in range(TILES)]
+        for i in range(TILES):
+            half, sub = divmod(i, BANK // P)
             ln = sb("ln%d" % i, [P, S2], F32)
             nc.scalar.activation(out=ln[:], in_=sig[i][:], func=ACT.Ln, bias=ln_floor[:])
-            lc = sb("lc%d" % i, [P, S2], F32)
-            nc.vector.tensor_scalar(out=lc[:], in0=ln[:], scalar1=-SQRT_FLOOR, scalar2=None, op0=ALU.min)
             u = sb("neg_soft%d" % i, [P, S2], F32)
-            nc.vector.scalar_tensor_tensor(out=u[:], in0=z_ps[i][:], scalar=neg_temp[:, i : i + 1], in1=lc[:], op0=ALU.mult, op1=ALU.min)
-            neg_soft.append(u)
+            nc.vector.tensor_tensor(out=u[:], in0=neg_relu[i][:], in1=ln[:], op=ALU.min)
+            for q in range(S2 // P):
+                nc.tensor.transpose(o_ps[PACK * half + q][:, P * sub : P * (sub + 1)], u[:, P * q : P * (q + 1)], ident[:])
 
-        for pair in range(S // PAIR):
-            for b in range(2):
-                o_ps = bank("o_ps%d_%d" % (pair, b), 2 * pair + b)
-                for sub in range(2):
-                    for q in range(2):
-                        nc.tensor.transpose(
-                            o_ps[:, PAIR * q + P * sub : PAIR * q + P * (sub + 1)],
-                            neg_soft[2 * pair + sub][:, P * (2 * b + q) : P * (2 * b + q + 1)],
-                            ident[:],
-                        )
-                res = sb("res%d_%d" % (pair, b), [P, 2, PAIR], F32)
-                nc.scalar.activation(out=res[:].rearrange("p q j -> p (q j)"), in_=o_ps[:], func=ACT.Sqrt, scale=-1.0)
-                nc.sync.dma_start(
-                    out=out[PAIR * b : PAIR * (b + 1), PAIR * pair : PAIR * (pair + 1)].rearrange("(q p) j -> p q j", p=P), in_=res[:]
-                )
+        for half in range(HALVES):
+            for q in range(S2 // P):
+                res = sb("res%d_%d" % (half, q), [P, BANK], F32)
+                nc.scalar.activation(out=res[:], in_=o_ps[PACK * half + q][:], func=ACT.Sqrt, scale=-1.0)
+                nc.sync.dma_start(out=out[P * q : P * (q + 1), half_cols(half)], in_=res[:])

@@ -194,11 +194,11 @@ def tile_list_expert_routing_affinities_kernel(
         move_scale_rows(nc.sync, 0, slice(0, S))
         load_w1(nc.sync, 1, 0, H)
         load_v(nc.sync, 1)
-        nc.sync.dma_start(out=bias[:], in_=b1.rearrange("(p t) -> p t", t=PACK))
         nc.sync.dma_start(experts[:], offs2)
         move_scale_rows(nc.sync, 1, slice(0, S))
-        load_scale_rows(nc.sync, lambda live: c_scale_tab[live, :], lambda rows: tab2_scales[0, rows, :])
         nc.sync.dma_start(out=c_word_tab[:], in_=tab2_words[0].rearrange("p t i -> p (t i)").bitcast(I32))
+        load_scale_rows(nc.sync, lambda live: c_scale_tab[live, :], lambda rows: tab2_scales[0, rows, :])
+        nc.sync.dma_start(out=bias[:], in_=b1.rearrange("(p t) -> p t", t=PACK))
         nc.vector.tensor_copy(
             out=w4_codes[:].bitcast(U16).rearrange("p a (t m) -> p a t m", t=PACK),
             in_=w4_raw[:].bitcast(U16).rearrange("p a (m t) -> p a t m", t=PACK),
@@ -231,15 +231,10 @@ def tile_list_expert_routing_affinities_kernel(
         finish_half(0, True)
         gather_words(1, 1)
         finish_half(1, True)
-        nc.vector.tensor_copy(out=c_plane[:], in_=c_scale_tab[:].bitcast(U8).indirect(experts[:]))
         nc.vector.tensor_copy(out=c_words[:], in_=c_word_tab[:].bitcast(U32).indirect(experts[:]))
-        score(PAIR * 0, P)
-        score(PAIR * 0 + P, P)
-        score(PAIR * 1, PAIR)
-        score(PAIR * 2, P)
-        score(PAIR * 2 + P, P)
-        score(PAIR * 3, P)
-        score(PAIR * 3 + P, P)
+        nc.vector.tensor_copy(out=c_plane[:], in_=c_scale_tab[:].bitcast(U8).indirect(experts[:]))
+        for i in range(TILES):
+            score(P * i, P)
 
         ln_floor = sb("ln_floor", [P, 1], F32)
         nc.gpsimd.tensor_scalar(out=ln_floor[:], in0=sig[TILES - 2][:, 0:1], scalar1=0.0, scalar2=LN_FLOOR, op0=ALU.mult, op1=ALU.add)

@@ -23,10 +23,13 @@ PASSES = K // (P * PACK)
 BANK = 512
 HALVES = S // BANK
 TILES = S // P
-PAIR = 2 * P
+QUADS = 4
+LIVE = 4
+LIST_ROWS = 16
+RUN = 4
+SCALAR_SHARE = H // 2
 LN_FLOOR = 2.0**-60
 SQRT_FLOOR = 2.0**-100
-VECTOR_PLANES = []
 
 
 def tile_list_expert_routing_affinities_kernel(
@@ -38,15 +41,15 @@ def tile_list_expert_routing_affinities_kernel(
         keep = ctx.enter_context(tc.tile_pool(name="keep", bufs=1))
         psum = ctx.enter_context(tc.psum_pool(name="psum", bufs=1))
 
-        def sb(name, shape, dtype):
-            return keep.tile(shape, dtype, name=name, align_bytes=64)
+        def sb(name, shape, dtype, tag=None):
+            return keep.tile(shape, dtype, name=name, tag=tag or name, align_bytes=64)
 
         def bank(name, b):
             return psum.tile([P, BANK], F32, name=name, tag="bank%d" % b)
 
-        tokens = lists.tile([P, S // 16], U16, name="tokens")
-        experts = lists.tile([P, S2 // 16], U16, name="experts")
-        v_scale_tab = [sb("v_scale_tab%d" % a, [P, T // 4], I32) for a in range(1)]
+        tokens = lists.tile([P, S // LIST_ROWS], U16, name="tokens")
+        experts = lists.tile([P, S2 // LIST_ROWS], U16, name="experts")
+        v_scale_tab = sb("v_scale_tab", [P, T // 4], I32)
         w4_scale_raw = sb("w4_scale_raw", [P, PASSES, H // 4], I32)
         c_scale_tab = sb("c_scale_tab", [P, T2 // 4], I32)
         neg_temp = sb("neg_temp", [P, TILES], F32)
@@ -61,15 +64,15 @@ def tile_list_expert_routing_affinities_kernel(
         w4_planes = sb("w4_planes", [P, PASSES, H], U8)
         v_words = [sb("v_words%d" % a, [P, S], U32) for a in range(PASSES)]
         v_scales = sb("v_scales", [P, S], U8)
-        v_plane_pair = sb("v_plane_pair", [P, PASSES, S], U8)
-        v_planes = [v_plane_pair[:, a, :] for a in range(PASSES)]
+        v_planes = sb("v_planes", [P, PASSES, S], U8)
         temp_rows = sb("temp_rows", [P, P], F32)
         c_words = sb("c_words", [P, S2], U32)
         c_plane = sb("c_plane", [P, S2], U8)
         w1_bf = [sb("w1_bf%d" % a, [P, PACK * H], BF16) for a in range(PASSES)]
         w1_codes = [sb("w1_codes%d" % a, [P, H], U32) for a in range(PASSES)]
         w1_planes = [sb("w1_planes%d" % a, [P, H], U8) for a in range(PASSES)]
-        h_planes = [sb("h_planes%d" % half, [P, PACK, BANK], BF16) for half in range(HALVES)]
+        h_rows = [sb("h_rows%d" % half, [P, PACK, BANK], BF16) for half in range(HALVES)]
+        h_woven = sb("h_woven", [P, TILES, P * PACK], BF16, tag="woven_then_relu")
         h_ps = [[bank("h_ps0_%d" % t, t) for t in range(PACK)]]
         z_ps = []
         sig = []
@@ -77,31 +80,30 @@ def tile_list_expert_routing_affinities_kernel(
         def half_cols(half):
             return slice(BANK * half, BANK * (half + 1))
 
-        def half_list(half):
-            return tokens[:, (BANK // 16) * half : (BANK // 16) * (half + 1)]
+        def tile_cols(i):
+            return slice(P * i, P * (i + 1))
+
+        def live_rows(quad):
+            return slice(32 * quad, 32 * quad + LIVE)
 
         def load_scale_rows(engine, plane, rows_of):
-            for quad in range(4):
-                engine.dma_start(out=plane(slice(32 * quad, 32 * quad + 4)), in_=rows_of(slice(4 * quad, 4 * quad + 4)).bitcast(I32))
+            for quad in range(QUADS):
+                engine.dma_start(out=plane(live_rows(quad)), in_=rows_of(slice(LIVE * quad, LIVE * (quad + 1))).bitcast(I32))
 
-        def load_w1(engine, a, c0, c1):
-            engine.dma_start(out=w1_raw[a][:, :, c0:c1], in_=w1[512 * a : 512 * (a + 1), c0:c1].rearrange("(p j) c -> p j c", j=PACK))
+        def load_w1(a):
+            nc.sync.dma_start(out=w1_raw[a][:], in_=w1[P * PACK * a : P * PACK * (a + 1), :].rearrange("(p j) c -> p j c", j=PACK))
 
-        def load_v(engine, a):
-            engine.dma_start(out=v_word_tab[a][:], in_=tab_words[a].rearrange("p t i -> p (t i)").bitcast(I32))
-
-        def gather_scales(a, half):
-            nc.vector.tensor_copy(out=v_scales[:, half_cols(half)], in_=v_scale_tab[a][:].bitcast(U8).indirect(half_list(half)))
+        def load_words(tile, words):
+            nc.sync.dma_start(out=tile[:], in_=words.rearrange("p t i -> p (t i)").bitcast(I32))
 
         def gather_words(a, half):
-            nc.vector.tensor_copy(out=v_words[a][:, half_cols(half)], in_=v_word_tab[a][:].bitcast(U32).indirect(half_list(half)))
+            picks = tokens[:, (BANK // LIST_ROWS) * half : (BANK // LIST_ROWS) * (half + 1)]
+            nc.vector.tensor_copy(out=v_words[a][:, half_cols(half)], in_=v_word_tab[a][:].bitcast(U32).indirect(picks))
 
-        def move_scale_rows(engine, a, cols):
-            for quad in range(4):
-                first = 16 * a + 4 * quad
-                engine.dma_start(
-                    out=v_planes[a][32 * quad : 32 * quad + 4, cols].bitcast(I32), in_=v_scales[first : first + 4, cols].bitcast(I32)
-                )
+        def move_scale_rows(a):
+            for quad in range(QUADS):
+                first = QUADS * LIVE * a + LIVE * quad
+                nc.sync.dma_start(out=v_planes[live_rows(quad), a, :].bitcast(I32), in_=v_scales[first : first + LIVE, :].bitcast(I32))
 
         def round_w1(copy, a, c0, c1):
             copy(
@@ -110,15 +112,17 @@ def tile_list_expert_routing_affinities_kernel(
             )
 
         def quantize_w1(a):
+            round_w1(nc.scalar.copy, a, 0, SCALAR_SHARE)
+            round_w1(nc.vector.tensor_copy, a, SCALAR_SHARE, H)
             nc.vector.quantize_mx(out=w1_codes[a][:].bitcast(FP8X4), scales=w1_planes[a][:], in_=w1_bf[a][:])
 
         def pass_w4(a, half, t):
             nc.tensor.matmul_mx(
                 out=h_ps[half][t][:],
                 lhsT=w4_codes[:, a, 2 * P * t : 2 * P * (t + 1)].bitcast(FP4X4),
-                lhsT_scale=w4_planes[:, a, P * t : P * (t + 1)],
+                lhsT_scale=w4_planes[:, a, tile_cols(t)],
                 rhs=v_words[a][:, half_cols(half)].bitcast(FP8X4),
-                rhs_scale=v_planes[a][:, half_cols(half)],
+                rhs_scale=v_planes[:, a, half_cols(half)],
                 start=(a == 0),
                 stop=False,
             )
@@ -126,79 +130,65 @@ def tile_list_expert_routing_affinities_kernel(
         def pass_w1(a, half, t):
             nc.tensor.matmul_mx(
                 out=h_ps[half][t][:],
-                lhsT=w1_codes[a][:, P * t : P * (t + 1)].bitcast(FP8X4),
-                lhsT_scale=w1_planes[a][:, P * t : P * (t + 1)],
+                lhsT=w1_codes[a][:, tile_cols(t)].bitcast(FP8X4),
+                lhsT_scale=w1_planes[a][:, tile_cols(t)],
                 rhs=v_words[a][:, half_cols(half)].bitcast(FP8X4),
-                rhs_scale=v_planes[a][:, half_cols(half)],
+                rhs_scale=v_planes[:, a, half_cols(half)],
                 start=False,
                 stop=(a == PASSES - 1),
             )
 
-        def leave_bank(half, t):
-            if (half, t) in VECTOR_PLANES:
-                nc.vector.tensor_scalar(out=h_planes[half][:, t, :], in0=h_ps[half][t][:], scalar1=bias[:, t : t + 1], scalar2=None, op0=ALU.add)
-            else:
-                nc.scalar.activation(out=h_planes[half][:, t, :], in_=h_ps[half][t][:], func=ACT.Identity, bias=bias[:, t : t + 1])
-
-        def finish_half(half, with_w4):
-            for t in range(PACK):
-                if with_w4:
-                    pass_w4(1, half, t)
-                pass_w1(1, half, t)
-                leave_bank(half, t)
-
-        def score(first_token, width):
-            half, first = divmod(first_token, BANK)
-            h_bf = sb("h_bf%d" % first_token, [P, width, PACK], BF16)
+        def score(i):
+            half, sub = divmod(i, BANK // P)
             nc.vector.tensor_copy(
-                out=h_bf[:].rearrange("p (c i) t -> p c t i", i=4),
-                in_=h_planes[half][:, :, first : first + width].rearrange("p t (c i) -> p c t i", i=4),
+                out=h_woven[:, i, :].rearrange("p (c n t) -> p c t n", n=RUN, t=PACK),
+                in_=h_rows[half][:, :, tile_cols(sub)].rearrange("p t (c n) -> p c t n", n=RUN),
             )
-            h_codes = sb("h_codes%d" % first_token, [P, width], U32)
-            h_plane = sb("h_plane%d" % first_token, [P, width], U8)
-            nc.vector.quantize_mx(out=h_codes[:].bitcast(FP8X4), scales=h_plane[:], in_=h_bf[:].rearrange("p n t -> p (n t)"))
-            for sub in range(width // P):
-                i = first_token // P + sub
-                z = bank("z_ps%d" % i, i)
-                nc.tensor.matmul_mx(
-                    out=z[:],
-                    lhsT=h_codes[:, P * sub : P * (sub + 1)].bitcast(FP8X4),
-                    lhsT_scale=h_plane[:, P * sub : P * (sub + 1)],
-                    rhs=c_words[:].bitcast(FP8X4),
-                    rhs_scale=c_plane[:],
-                    start=True,
-                    stop=True,
-                )
-                s = sb("sig%d" % i, [P, S2], F32)
-                nc.scalar.activation(out=s[:], in_=z[:], func=ACT.Sigmoid, scale=neg_temp[:, i : i + 1])
-                z_ps.append(z)
-                sig.append(s)
+            h_codes = sb("h_codes%d" % i, [P, P], U32)
+            h_plane = sb("h_plane%d" % i, [P, P], U8)
+            nc.vector.quantize_mx(out=h_codes[:].bitcast(FP8X4), scales=h_plane[:], in_=h_woven[:, i, :])
+            z = bank("z_ps%d" % i, i)
+            nc.tensor.matmul_mx(
+                out=z[:],
+                lhsT=h_codes[:].bitcast(FP8X4),
+                lhsT_scale=h_plane[:],
+                rhs=c_words[:].bitcast(FP8X4),
+                rhs_scale=c_plane[:],
+                start=True,
+                stop=True,
+            )
+            s = sb("sig%d" % i, [P, S2], F32)
+            nc.scalar.activation(out=s[:], in_=z[:], func=ACT.Sigmoid, scale=neg_temp[:, i : i + 1])
+            z_ps.append(z)
+            sig.append(s)
 
         nc.gpsimd.memset(warm[:], 0.0)
         nc.scalar.activation(out=warm[:, 1:2], in_=warm[:, 0:1], func=ACT.Sigmoid)
-        nc.vector.memset(v_scale_tab[0][32:64, :], 0)
-        nc.vector.memset(v_scale_tab[0][64:128, :], 0)
+        nc.vector.memset(v_scale_tab[32:64, :], 0)
+        nc.vector.memset(v_scale_tab[64:P, :], 0)
         nc.gpsimd.memset(w4_scale_raw[:], 0)
         nc.gpsimd.memset(temp_rows[:], 0.0)
-        nc.gpsimd.memset(v_plane_pair[:].bitcast(I32), 0)
+        nc.gpsimd.memset(v_planes[:].bitcast(I32), 0)
         nc.gpsimd.memset(c_scale_tab[:], 0)
         make_identity(nc, ident[:])
-        nc.sync.dma_start(out=v_scale_tab[0][0:32, :], in_=tab_scales.rearrange("a q t -> (a q) t").bitcast(I32))
+
+        nc.sync.dma_start(out=v_scale_tab[0:32, :], in_=tab_scales.rearrange("a q t -> (a q) t").bitcast(I32))
         nc.sync.dma_start(tokens[:], offs)
         nc.sync.dma_start(out=w4_raw[:], in_=w4_words.rearrange("a p n -> p a n").bitcast(I32))
-        load_v(nc.sync, 0)
-        load_w1(nc.sync, 0, 0, H)
+        load_words(v_word_tab[0], tab_words[0])
+        load_w1(0)
         load_scale_rows(nc.scalar, lambda live: w4_scale_raw[live, :, :], lambda rows: w4_scales[:, rows, :].rearrange("a r n -> r a n"))
         nc.scalar.dma_start(out=temp_rows[0:TILES, :], in_=temp.rearrange("(i p) -> i p", p=P))
-        nc.vector.tensor_copy(out=v_scales[:], in_=v_scale_tab[0][:].bitcast(U8).indirect(tokens[:]))
-        move_scale_rows(nc.sync, 0, slice(0, S))
-        load_w1(nc.sync, 1, 0, H)
-        load_v(nc.sync, 1)
+        nc.vector.tensor_copy(out=v_scales[:], in_=v_scale_tab[:].bitcast(U8).indirect(tokens[:]))
+        move_scale_rows(0)
+        load_w1(1)
+        load_words(v_word_tab[1], tab_words[1])
         nc.sync.dma_start(experts[:], offs2)
-        move_scale_rows(nc.sync, 1, slice(0, S))
-        nc.sync.dma_start(out=c_word_tab[:], in_=tab2_words[0].rearrange("p t i -> p (t i)").bitcast(I32))
+        move_scale_rows(1)
+        load_words(c_word_tab, tab2_words[0])
         load_scale_rows(nc.sync, lambda live: c_scale_tab[live, :], lambda rows: tab2_scales[0, rows, :])
         nc.sync.dma_start(out=bias[:], in_=b1.rearrange("(p t) -> p t", t=PACK))
+
         nc.vector.tensor_copy(
             out=w4_codes[:].bitcast(U16).rearrange("p a (t m) -> p a t m", t=PACK),
             in_=w4_raw[:].bitcast(U16).rearrange("p a (m t) -> p a t m", t=PACK),
@@ -207,56 +197,53 @@ def tile_list_expert_routing_affinities_kernel(
             out=w4_planes[:].rearrange("p a (t m) -> p a t m", t=PACK),
             in_=w4_scale_raw[:].bitcast(U8).rearrange("p a (m t) -> p a t m", t=PACK),
         )
-        temp_ps = bank("temp_ps", 7)
+        temp_ps = bank("temp_ps", TILES - 1)
         nc.tensor.transpose(temp_ps[:, 0:P], temp_rows[:], ident[:])
         nc.scalar.activation(out=neg_temp[:], in_=temp_ps[:, 0:TILES], func=ACT.Copy, scale=-1.0)
         h_ps.append([bank("h_ps1_%d" % t, PACK + t) for t in range(PACK)])
-        gather_words(0, 0)
-        for t in range(PACK):
-            pass_w4(0, 0, t)
-        gather_words(0, 1)
-        for t in range(PACK):
-            pass_w4(0, 1, t)
-        round_w1(nc.scalar.copy, 0, 0, H // 2)
-        round_w1(nc.vector.tensor_copy, 0, H // 2, H)
+
+        for half in range(HALVES):
+            gather_words(0, half)
+            for t in range(PACK):
+                pass_w4(0, half, t)
         quantize_w1(0)
-        for t in range(PACK):
-            pass_w1(0, 0, t)
-        for t in range(PACK):
-            pass_w1(0, 1, t)
-        round_w1(nc.scalar.copy, 1, 0, H // 2)
-        round_w1(nc.vector.tensor_copy, 1, H // 2, H)
+        for half in range(HALVES):
+            for t in range(PACK):
+                pass_w1(0, half, t)
         quantize_w1(1)
-        gather_words(1, 0)
-        finish_half(0, True)
-        gather_words(1, 1)
-        finish_half(1, True)
+        for half in range(HALVES):
+            gather_words(1, half)
+            for t in range(PACK):
+                pass_w4(1, half, t)
+                pass_w1(1, half, t)
+                nc.scalar.activation(out=h_rows[half][:, t, :], in_=h_ps[half][t][:], func=ACT.Identity, bias=bias[:, t : t + 1])
+
         nc.vector.tensor_copy(out=c_words[:], in_=c_word_tab[:].bitcast(U32).indirect(experts[:]))
         nc.vector.tensor_copy(out=c_plane[:], in_=c_scale_tab[:].bitcast(U8).indirect(experts[:]))
         for i in range(TILES):
-            score(P * i, P)
+            score(i)
 
         ln_floor = sb("ln_floor", [P, 1], F32)
         nc.gpsimd.tensor_scalar(out=ln_floor[:], in0=sig[TILES - 2][:, 0:1], scalar1=0.0, scalar2=LN_FLOOR, op0=ALU.mult, op1=ALU.add)
 
-        neg_relu = []
+        neg_relu = sb("neg_relu", [P, TILES, S2], F32, tag="woven_then_relu")
         for i in range(TILES):
-            nz = sb("neg_relu%d" % i, [P, S2], F32)
-            nc.vector.tensor_scalar(out=nz[:], in0=z_ps[i][:], scalar1=neg_temp[:, i : i + 1], scalar2=-SQRT_FLOOR, op0=ALU.mult, op1=ALU.min)
-            neg_relu.append(nz)
+            nc.vector.tensor_scalar(
+                out=neg_relu[:, i, :], in0=z_ps[i][:], scalar1=neg_temp[:, i : i + 1], scalar2=-SQRT_FLOOR, op0=ALU.mult, op1=ALU.min
+            )
 
         o_ps = [bank("o_ps%d" % b, b) for b in range(TILES)]
         for i in range(TILES):
             half, sub = divmod(i, BANK // P)
             ln = sb("ln%d" % i, [P, S2], F32)
             nc.scalar.activation(out=ln[:], in_=sig[i][:], func=ACT.Ln, bias=ln_floor[:])
-            u = sb("neg_soft%d" % i, [P, S2], F32)
-            nc.vector.tensor_tensor(out=u[:], in0=neg_relu[i][:], in1=ln[:], op=ALU.min)
+            neg_soft = sb("neg_soft%d" % i, [P, S2], F32)
+            nc.vector.tensor_tensor(out=neg_soft[:], in0=neg_relu[:, i, :], in1=ln[:], op=ALU.min)
             for q in range(S2 // P):
-                nc.tensor.transpose(o_ps[PACK * half + q][:, P * sub : P * (sub + 1)], u[:, P * q : P * (q + 1)], ident[:])
+                nc.tensor.transpose(o_ps[PACK * half + q][:, tile_cols(sub)], neg_soft[:, tile_cols(q)], ident[:])
 
         for half in range(HALVES):
             for q in range(S2 // P):
                 res = sb("res%d_%d" % (half, q), [P, BANK], F32)
                 nc.scalar.activation(out=res[:], in_=o_ps[PACK * half + q][:], func=ACT.Sqrt, scale=-1.0)
-                nc.sync.dma_start(out=out[P * q : P * (q + 1), half_cols(half)], in_=res[:])
+                nc.sync.dma_start(out=out[tile_cols(q), half_cols(half)], in_=res[:])

@@ -233,17 +233,19 @@ def tile_list_expert_routing_affinities_kernel(
             )
 
         o_ps = [bank("o_ps%d" % b, b) for b in range(TILES)]
+        neg_soft = []
         for i in range(TILES):
-            half, sub = divmod(i, BANK // P)
             ln = sb("ln%d" % i, [P, S2], F32)
             nc.scalar.activation(out=ln[:], in_=sig[i][:], func=ACT.Ln, bias=ln_floor[:])
-            neg_soft = sb("neg_soft%d" % i, [P, S2], F32)
-            nc.vector.tensor_tensor(out=neg_soft[:], in0=neg_relu[:, i, :], in1=ln[:], op=ALU.min)
-            for q in range(S2 // P):
-                nc.tensor.transpose(o_ps[PACK * half + q][:, tile_cols(sub)], neg_soft[:, tile_cols(q)], ident[:])
+            neg_soft.append(sb("neg_soft%d" % i, [P, S2], F32))
+            nc.vector.tensor_tensor(out=neg_soft[i][:], in0=neg_relu[:, i, :], in1=ln[:], op=ALU.min)
+        for q in range(S2 // P):
+            for i in range(TILES):
+                half, sub = divmod(i, BANK // P)
+                nc.tensor.transpose(o_ps[PACK * half + q][:, tile_cols(sub)], neg_soft[i][:, tile_cols(q)], ident[:])
 
-        for half in range(HALVES):
-            for q in range(S2 // P):
+        for q in range(S2 // P):
+            for half in range(HALVES):
                 res = sb("res%d_%d" % (half, q), [P, BANK], F32)
                 nc.scalar.activation(out=res[:], in_=o_ps[PACK * half + q][:], func=ACT.Sqrt, scale=-1.0)
                 nc.sync.dma_start(out=out[tile_cols(q), half_cols(half)], in_=res[:])

@@ -28,6 +28,7 @@ LIVE = 4
 LIST_ROWS = 16
 RUN = 4
 SCALAR_SHARE = H // 2
+VECTOR_TILES = 2
 LN_FLOOR = 2.0**-60
 SQRT_FLOOR = 2.0**-100
 
@@ -216,11 +217,18 @@ def tile_list_expert_routing_affinities_kernel(
             for t in range(PACK):
                 pass_w4(1, half, t)
                 pass_w1(1, half, t)
-                nc.scalar.activation(out=h_rows[half][:, t, :], in_=h_ps[half][t][:], func=ACT.Identity, bias=bias[:, t : t + 1])
+                last = half == HALVES - 1 and t == PACK - 1
+                cols = slice(0, BANK - VECTOR_TILES * P if last else BANK)
+                nc.scalar.activation(out=h_rows[half][:, t, cols], in_=h_ps[half][t][:, cols], func=ACT.Identity, bias=bias[:, t : t + 1])
 
         nc.vector.tensor_copy(out=c_words[:], in_=c_word_tab[:].bitcast(U32).indirect(experts[:]))
         nc.vector.tensor_copy(out=c_plane[:], in_=c_scale_tab[:].bitcast(U8).indirect(experts[:]))
         for i in range(TILES):
+            if i == TILES - VECTOR_TILES:
+                cols = slice(BANK - VECTOR_TILES * P, BANK)
+                nc.vector.tensor_scalar(
+                    out=h_rows[-1][:, PACK - 1, cols], in0=h_ps[-1][-1][:, cols], scalar1=bias[:, PACK - 1 : PACK], scalar2=None, op0=ALU.add
+                )
             score(i)
 
         ln_floor = sb("ln_floor", [P, 1], F32)

@@ -29,6 +29,7 @@ LIST_ROWS = 16
 RUN = 4
 SCALAR_SHARE = H // 2
 VECTOR_TILES = 2
+LN_TILES = BANK // P
 LN_FLOOR = 2.0**-60
 SQRT_FLOOR = 2.0**-100
 
@@ -75,8 +76,9 @@ def tile_list_expert_routing_affinities_kernel(
         h_rows = [sb("h_rows%d" % half, [P, PACK, BANK], BF16) for half in range(HALVES)]
         h_woven = sb("h_woven", [P, TILES, P * PACK], BF16, tag="woven_then_relu")
         h_ps = [[bank("h_ps0_%d" % t, t) for t in range(PACK)]]
+        sig = sb("sig", [P, TILES, S2], F32)
+        ln = sb("ln", [P, TILES, S2], F32)
         z_ps = []
-        sig = []
 
         def half_cols(half):
             return slice(BANK * half, BANK * (half + 1))
@@ -158,10 +160,8 @@ def tile_list_expert_routing_affinities_kernel(
                 start=True,
                 stop=True,
             )
-            s = sb("sig%d" % i, [P, S2], F32)
-            nc.scalar.activation(out=s[:], in_=z[:], func=ACT.Sigmoid, scale=neg_temp[:, i : i + 1])
+            nc.scalar.activation(out=sig[:, i, :], in_=z[:], func=ACT.Sigmoid, scale=neg_temp[:, i : i + 1])
             z_ps.append(z)
-            sig.append(s)
 
         nc.gpsimd.memset(warm[:], 0.0)
         nc.scalar.activation(out=warm[:, 1:2], in_=warm[:, 0:1], func=ACT.Sigmoid)
@@ -232,7 +232,7 @@ def tile_list_expert_routing_affinities_kernel(
             score(i)
 
         ln_floor = sb("ln_floor", [P, 1], F32)
-        nc.gpsimd.tensor_scalar(out=ln_floor[:], in0=sig[TILES - 2][:, 0:1], scalar1=0.0, scalar2=LN_FLOOR, op0=ALU.mult, op1=ALU.add)
+        nc.gpsimd.tensor_scalar(out=ln_floor[:], in0=sig[:, TILES - 2, 0:1], scalar1=0.0, scalar2=LN_FLOOR, op0=ALU.mult, op1=ALU.add)
 
         neg_relu = sb("neg_relu", [P, TILES, S2], F32, tag="woven_then_relu")
         for i in range(TILES):
@@ -243,17 +243,17 @@ def tile_list_expert_routing_affinities_kernel(
         o_ps = [bank("o_ps%d" % b, b) for b in range(TILES)]
         neg_soft = []
         for i in range(TILES):
-            ln = sb("ln%d" % i, [P, S2], F32)
-            nc.scalar.activation(out=ln[:], in_=sig[i][:], func=ACT.Ln, bias=ln_floor[:])
+            if i % LN_TILES == 0:
+                group = slice(i, i + LN_TILES)
+                nc.scalar.activation(out=ln[:, group, :], in_=sig[:, group, :], func=ACT.Ln, bias=ln_floor[:])
             neg_soft.append(sb("neg_soft%d" % i, [P, S2], F32))
-            nc.vector.tensor_tensor(out=neg_soft[i][:], in0=neg_relu[:, i, :], in1=ln[:], op=ALU.min)
-        for q in range(S2 // P):
-            for i in range(TILES):
-                half, sub = divmod(i, BANK // P)
+            nc.vector.tensor_tensor(out=neg_soft[i][:], in0=neg_relu[:, i, :], in1=ln[:, i, :], op=ALU.min)
+            half, sub = divmod(i, BANK // P)
+            for q in range(S2 // P):
                 nc.tensor.transpose(o_ps[PACK * half + q][:, tile_cols(sub)], neg_soft[i][:, tile_cols(q)], ident[:])
 
-        for q in range(S2 // P):
-            for half in range(HALVES):
+        for half in range(HALVES):
+            for q in range(S2 // P):
                 res = sb("res%d_%d" % (half, q), [P, BANK], F32)
                 nc.scalar.activation(out=res[:], in_=o_ps[PACK * half + q][:], func=ACT.Sqrt, scale=-1.0)
                 nc.sync.dma_start(out=out[tile_cols(q), half_cols(half)], in_=res[:])

@@ -30,6 +30,8 @@ RUN = 4
 SCALAR_SHARE = H // 2
 VECTOR_TILES = 2
 LN_TILES = BANK // P
+PIECE = BANK // 2
+SPLIT_BANKS = 2
 LN_FLOOR = 2.0**-60
 SQRT_FLOOR = 2.0**-100
 
@@ -99,9 +101,9 @@ def tile_list_expert_routing_affinities_kernel(
         def load_words(tile, words):
             nc.sync.dma_start(out=tile[:], in_=words.rearrange("p t i -> p (t i)").bitcast(I32))
 
-        def gather_words(a, half):
-            picks = tokens[:, (BANK // LIST_ROWS) * half : (BANK // LIST_ROWS) * (half + 1)]
-            nc.vector.tensor_copy(out=v_words[a][:, half_cols(half)], in_=v_word_tab[a][:].bitcast(U32).indirect(picks))
+        def gather_words(a, cols):
+            picks = tokens[:, cols.start // LIST_ROWS : cols.stop // LIST_ROWS]
+            nc.vector.tensor_copy(out=v_words[a][:, cols], in_=v_word_tab[a][:].bitcast(U32).indirect(picks))
 
         def move_scale_rows(a):
             for quad in range(QUADS):
@@ -119,26 +121,28 @@ def tile_list_expert_routing_affinities_kernel(
             round_w1(nc.vector.tensor_copy, a, SCALAR_SHARE, H)
             nc.vector.quantize_mx(out=w1_codes[a][:].bitcast(FP8X4), scales=w1_planes[a][:], in_=w1_bf[a][:])
 
-        def pass_w4(a, half, t):
+        def pass_w4(a, half, t, part=slice(0, BANK)):
+            cols = slice(BANK * half + part.start, BANK * half + part.stop)
             nc.tensor.matmul_mx(
-                out=h_ps[half][t][:],
+                out=h_ps[half][t][:, part],
                 lhsT=w4_codes[:, a, 2 * P * t : 2 * P * (t + 1)].bitcast(FP4X4),
                 lhsT_scale=w4_planes[:, a, tile_cols(t)],
-                rhs=v_words[a][:, half_cols(half)].bitcast(FP8X4),
-                rhs_scale=v_planes[:, a, half_cols(half)],
+                rhs=v_words[a][:, cols].bitcast(FP8X4),
+                rhs_scale=v_planes[:, a, cols],
                 start=(a == 0),
                 stop=False,
             )
 
-        def pass_w1(a, half, t):
+        def pass_w1(a, half, t, part=slice(0, BANK)):
+            cols = slice(BANK * half + part.start, BANK * half + part.stop)
             nc.tensor.matmul_mx(
-                out=h_ps[half][t][:],
+                out=h_ps[half][t][:, part],
                 lhsT=w1_codes[a][:, tile_cols(t)].bitcast(FP8X4),
                 lhsT_scale=w1_planes[a][:, tile_cols(t)],
-                rhs=v_words[a][:, half_cols(half)].bitcast(FP8X4),
-                rhs_scale=v_planes[:, a, half_cols(half)],
+                rhs=v_words[a][:, cols].bitcast(FP8X4),
+                rhs_scale=v_planes[:, a, cols],
                 start=False,
-                stop=(a == PASSES - 1),
+                stop=(a == PASSES - 1 and part.stop == BANK),
             )
 
         def score(i):
@@ -204,7 +208,7 @@ def tile_list_expert_routing_affinities_kernel(
         h_ps.append([bank("h_ps1_%d" % t, PACK + t) for t in range(PACK)])
 
         for half in range(HALVES):
-            gather_words(0, half)
+            gather_words(0, half_cols(half))
             for t in range(PACK):
                 pass_w4(0, half, t)
         quantize_w1(0)
@@ -212,11 +216,16 @@ def tile_list_expert_routing_affinities_kernel(
             for t in range(PACK):
                 pass_w1(0, half, t)
         quantize_w1(1)
+        gather_words(1, slice(0, PIECE))
+        for t in range(SPLIT_BANKS):
+            pass_w4(1, 0, t, slice(0, PIECE))
+            pass_w1(1, 0, t, slice(0, PIECE))
         for half in range(HALVES):
-            gather_words(1, half)
+            gather_words(1, slice(PIECE, BANK) if half == 0 else half_cols(half))
             for t in range(PACK):
-                pass_w4(1, half, t)
-                pass_w1(1, half, t)
+                part = slice(PIECE if half == 0 and t < SPLIT_BANKS else 0, BANK)
+                pass_w4(1, half, t, part)
+                pass_w1(1, half, t, part)
                 last = half == HALVES - 1 and t == PACK - 1
                 cols = slice(0, BANK - VECTOR_TILES * P if last else BANK)
                 nc.scalar.activation(out=h_rows[half][:, t, cols], in_=h_ps[half][t][:, cols], func=ACT.Identity, bias=bias[:, t : t + 1])

@@ -32,6 +32,7 @@ VECTOR_TILES = 2
 LN_TILES = BANK // P
 PIECE = BANK // 2
 SPLIT_BANKS = 2
+EDGE = BANK // 2
 LN_FLOOR = 2.0**-60
 SQRT_FLOOR = 2.0**-100
 
@@ -261,8 +262,10 @@ def tile_list_expert_routing_affinities_kernel(
             for q in range(S2 // P):
                 nc.tensor.transpose(o_ps[PACK * half + q][:, tile_cols(sub)], neg_soft[i][:, tile_cols(q)], ident[:])
 
-        for half in range(HALVES):
-            for q in range(S2 // P):
-                res = sb("res%d_%d" % (half, q), [P, BANK], F32)
-                nc.scalar.activation(out=res[:], in_=o_ps[PACK * half + q][:], func=ACT.Sqrt, scale=-1.0)
-                nc.sync.dma_start(out=out[tile_cols(q), half_cols(half)], in_=res[:])
+        for b in range(TILES):
+            half, q = divmod(b, S2 // P)
+            cuts = [0, EDGE, BANK] if b == 0 else [0, BANK - EDGE, BANK] if b == TILES - 1 else [0, BANK]
+            for c0, c1 in zip(cuts, cuts[1:]):
+                res = sb("res%d_%d" % (b, c0), [P, c1 - c0], F32)
+                nc.scalar.activation(out=res[:], in_=o_ps[b][:, c0:c1], func=ACT.Sqrt, scale=-1.0)
+                nc.sync.dma_start(out=out[tile_cols(q), BANK * half + c0 : BANK * half + c1], in_=res[:])

@@ -33,6 +33,8 @@ LN_TILES = BANK // P
 PIECE = BANK // 2
 SPLIT_BANKS = 2
 EDGE = BANK // 2
+LINE = 256
+MOVING, MOVING_SCALE, STILL, STILL_SCALE = 0, 64, 128, 192
 LN_FLOOR = 2.0**-60
 SQRT_FLOOR = 2.0**-100
 
@@ -48,6 +50,12 @@ def tile_list_expert_routing_affinities_kernel(
 
         def sb(name, shape, dtype, tag=None):
             return keep.tile(shape, dtype, name=name, tag=tag or name, align_bytes=64)
+
+        def mx(name, shape, dtype, size, shift):
+            pad = LINE // size
+            tile = keep.tile(shape[:-1] + [shape[-1] + pad], dtype, name=name, align_bytes=LINE)
+            cols = slice(shift // size, shift // size + shape[-1])
+            return tile[:, cols] if len(shape) == 2 else tile[:, :, cols]
 
         def bank(name, b):
             return psum.tile([P, BANK], F32, name=name, tag="bank%d" % b)
@@ -65,17 +73,17 @@ def tile_list_expert_routing_affinities_kernel(
         c_word_tab = sb("c_word_tab", [P, T2], I32)
         ident = sb("ident", [P, P], F32)
         warm = sb("warm", [P, 2], F32)
-        w4_codes = sb("w4_codes", [P, PASSES, 2 * H], U8)
-        w4_planes = sb("w4_planes", [P, PASSES, H], U8)
-        v_words = [sb("v_words%d" % a, [P, S], U32) for a in range(PASSES)]
+        w4_codes = mx("w4_codes", [P, PASSES, 2 * H], U8, 1, STILL)
+        w4_planes = mx("w4_planes", [P, PASSES, H], U8, 1, STILL_SCALE)
+        v_words = [mx("v_words%d" % a, [P, S], U32, 4, MOVING) for a in range(PASSES)]
         v_scales = sb("v_scales", [P, S], U8)
-        v_planes = sb("v_planes", [P, PASSES, S], U8)
+        v_planes = mx("v_planes", [P, PASSES, S], U8, 1, MOVING_SCALE)
         temp_rows = sb("temp_rows", [P, P], F32)
-        c_words = sb("c_words", [P, S2], U32)
-        c_plane = sb("c_plane", [P, S2], U8)
+        c_words = mx("c_words", [P, S2], U32, 4, MOVING)
+        c_plane = mx("c_plane", [P, S2], U8, 1, MOVING_SCALE)
         w1_bf = [sb("w1_bf%d" % a, [P, PACK * H], BF16) for a in range(PASSES)]
-        w1_codes = [sb("w1_codes%d" % a, [P, H], U32) for a in range(PASSES)]
-        w1_planes = [sb("w1_planes%d" % a, [P, H], U8) for a in range(PASSES)]
+        w1_codes = [mx("w1_codes%d" % a, [P, H], U32, 4, STILL) for a in range(PASSES)]
+        w1_planes = [mx("w1_planes%d" % a, [P, H], U8, 1, STILL_SCALE) for a in range(PASSES)]
         h_rows = [sb("h_rows%d" % half, [P, PACK, BANK], BF16) for half in range(HALVES)]
         h_woven = sb("h_woven", [P, TILES, P * PACK], BF16, tag="woven_then_relu")
         h_ps = [[bank("h_ps0_%d" % t, t) for t in range(PACK)]]
@@ -152,8 +160,8 @@ def tile_list_expert_routing_affinities_kernel(
                 out=h_woven[:, i, :].rearrange("p (c n t) -> p c t n", n=RUN, t=PACK),
                 in_=h_rows[half][:, :, tile_cols(sub)].rearrange("p t (c n) -> p c t n", n=RUN),
             )
-            h_codes = sb("h_codes%d" % i, [P, P], U32)
-            h_plane = sb("h_plane%d" % i, [P, P], U8)
+            h_codes = mx("h_codes%d" % i, [P, P], U32, 4, STILL)
+            h_plane = mx("h_plane%d" % i, [P, P], U8, 1, STILL_SCALE)
             nc.vector.quantize_mx(out=h_codes[:].bitcast(FP8X4), scales=h_plane[:], in_=h_woven[:, i, :])
             z = bank("z_ps%d" % i, i)
             nc.tensor.matmul_mx(

@@ -35,6 +35,7 @@ SPLIT_BANKS = 2
 EDGE = BANK // 2
 LINE = 256
 MOVING, MOVING_SCALE, STILL, STILL_SCALE = 0, 64, 128, 192
+WARM_PASSES = 3
 LN_FLOOR = 2.0**-60
 SQRT_FLOOR = 2.0**-100
 
@@ -214,6 +215,17 @@ def tile_list_expert_routing_affinities_kernel(
         temp_ps = bank("temp_ps", TILES - 1)
         nc.tensor.transpose(temp_ps[:, 0:P], temp_rows[:], ident[:])
         nc.scalar.activation(out=neg_temp[:], in_=temp_ps[:, 0:TILES], func=ACT.Copy, scale=-1.0)
+        warm_ps = bank("warm_ps", TILES - 2)
+        for t in range(WARM_PASSES):
+            nc.tensor.matmul_mx(
+                out=warm_ps[:],
+                lhsT=w4_raw[:, 0, P // 2 * t : P // 2 * (t + 1)].bitcast(U8).bitcast(FP4X4),
+                lhsT_scale=w4_scale_raw[:, 0, :].bitcast(U8)[:, tile_cols(t)],
+                rhs=v_word_tab[0][:, 0:BANK].bitcast(FP8X4),
+                rhs_scale=w4_scale_raw[:, 1, :].bitcast(U8),
+                start=True,
+                stop=True,
+            )
         h_ps.append([bank("h_ps1_%d" % t, PACK + t) for t in range(PACK)])
 
         for half in range(HALVES):

@@ -50,7 +50,7 @@ def tile_list_expert_routing_affinities_kernel(
         psum = ctx.enter_context(tc.psum_pool(name="psum", bufs=1))
 
         def sb(name, shape, dtype, tag=None):
-            return keep.tile(shape, dtype, name=name, tag=tag or name, align_bytes=64)
+            return keep.tile(shape, dtype, name=name, tag=tag or name, align_bytes=LINE)
 
         def mx(name, shape, dtype, size, shift):
             pad = LINE // size

@@ -36,6 +36,7 @@ EDGE = BANK // 2
 LINE = 256
 MOVING, MOVING_SCALE, STILL, STILL_SCALE = 0, 64, 128, 192
 WARM_PASSES = 3
+AHEAD = 1
 LN_FLOOR = 2.0**-60
 SQRT_FLOOR = 2.0**-100
 
@@ -105,8 +106,9 @@ def tile_list_expert_routing_affinities_kernel(
             for quad in range(QUADS):
                 engine.dma_start(out=plane(live_rows(quad)), in_=rows_of(slice(LIVE * quad, LIVE * (quad + 1))).bitcast(I32))
 
-        def load_w1(a):
-            nc.sync.dma_start(out=w1_raw[a][:], in_=w1[P * PACK * a : P * PACK * (a + 1), :].rearrange("(p j) c -> p j c", j=PACK))
+        def load_w1(a, j0, j1):
+            rows = w1[P * PACK * a : P * PACK * (a + 1), :].rearrange("(p j) c -> p j c", j=PACK)
+            nc.sync.dma_start(out=w1_raw[a][:, j0:j1, :], in_=rows[:, j0:j1, :])
 
         def load_words(tile, words):
             nc.sync.dma_start(out=tile[:], in_=words.rearrange("p t i -> p (t i)").bitcast(I32))
@@ -191,12 +193,13 @@ def tile_list_expert_routing_affinities_kernel(
         nc.sync.dma_start(tokens[:], offs)
         nc.sync.dma_start(out=w4_raw[:], in_=w4_words.rearrange("a p n -> p a n").bitcast(I32))
         load_words(v_word_tab[0], tab_words[0])
-        load_w1(0)
+        load_w1(0, 0, PACK)
+        load_w1(1, 0, AHEAD)
         load_scale_rows(nc.scalar, lambda live: w4_scale_raw[live, :, :], lambda rows: w4_scales[:, rows, :].rearrange("a r n -> r a n"))
         nc.scalar.dma_start(out=temp_rows[0:TILES, :], in_=temp.rearrange("(i p) -> i p", p=P))
         nc.vector.tensor_copy(out=v_scales[:], in_=v_scale_tab[:].bitcast(U8).indirect(tokens[:]))
         move_scale_rows(0)
-        load_w1(1)
+        load_w1(1, AHEAD, PACK)
         load_words(v_word_tab[1], tab_words[1])
         nc.sync.dma_start(experts[:], offs2)
         move_scale_rows(1)

from contextlib import ExitStack

import concourse.mybir as mybir
from concourse.masks import make_identity

K, H, T, S, T2, S2 = 1024, 512, 2048, 1024, 1024, 512
FLOPS = 2 * (2 * K * H * S + H * S2 * S)

F32 = mybir.dt.float32
BF16 = mybir.dt.bfloat16
I32 = mybir.dt.int32
U32 = mybir.dt.uint32
U16 = mybir.dt.uint16
U8 = mybir.dt.uint8
FP8X4 = mybir.dt.float8_e4m3fn_x4
FP4X4 = mybir.dt.float4_e2m1fn_x4
ACT = mybir.ActivationFunctionType
ALU = mybir.AluOpType

P = 128
PACK = 4
PASSES = K // (P * PACK)
BANK = 512
HALVES = S // BANK
TILES = S // P
QUADS = 4
LIVE = 4
LIST_ROWS = 16
RUN = 4
SCALAR_SHARE = H // 2
VECTOR_TILES = 2
LN_TILES = BANK // P
PIECE = BANK // 2
SPLIT_BANKS = 2
EDGE = BANK // 2
LINE = 256
MOVING, MOVING_SCALE, STILL, STILL_SCALE = 0, 64, 128, 192
WARM_PASSES = 3
AHEAD = 1
LN_FLOOR = 2.0**-60
SQRT_FLOOR = 2.0**-100


def tile_list_expert_routing_affinities_kernel(
    tc, tab_words, tab_scales, offs, tab2_words, tab2_scales, offs2, w4_words, w4_scales, w1, b1, temp, out
):
    nc = tc.nc
    with ExitStack() as ctx:
        lists = ctx.enter_context(tc.tile_pool(name="lists", bufs=1))
        keep = ctx.enter_context(tc.tile_pool(name="keep", bufs=1))
        psum = ctx.enter_context(tc.psum_pool(name="psum", bufs=1))

        def sb(name, shape, dtype, tag=None):
            return keep.tile(shape, dtype, name=name, tag=tag or name, align_bytes=LINE)

        def mx(name, shape, dtype, size, shift):
            pad = LINE // size
            tile = keep.tile(shape[:-1] + [shape[-1] + pad], dtype, name=name, align_bytes=LINE)
            cols = slice(shift // size, shift // size + shape[-1])
            return tile[:, cols] if len(shape) == 2 else tile[:, :, cols]

        def bank(name, b):
            return psum.tile([P, BANK], F32, name=name, tag="bank%d" % b)

        tokens = lists.tile([P, S // LIST_ROWS], U16, name="tokens")
        experts = lists.tile([P, S2 // LIST_ROWS], U16, name="experts")
        v_scale_tab = sb("v_scale_tab", [P, T // 4], I32)
        w4_scale_raw = sb("w4_scale_raw", [P, PASSES, H // 4], I32)
        c_scale_tab = sb("c_scale_tab", [P, T2 // 4], I32)
        neg_temp = sb("neg_temp", [P, TILES], F32)
        bias = sb("bias", [P, PACK], F32)
        w4_raw = sb("w4_raw", [P, PASSES, H // 2], I32)
        w1_raw = [sb("w1_raw%d" % a, [P, PACK, H], F32) for a in range(PASSES)]
        v_word_tab = [sb("v_word_tab%d" % a, [P, T], I32) for a in range(PASSES)]
        c_word_tab = sb("c_word_tab", [P, T2], I32)
        ident = sb("ident", [P, P], F32)
        warm = sb("warm", [P, 2], F32)
        w4_codes = mx("w4_codes", [P, PASSES, 2 * H], U8, 1, STILL)
        w4_planes = mx("w4_planes", [P, PASSES, H], U8, 1, STILL_SCALE)
        v_words = [mx("v_words%d" % a, [P, S], U32, 4, MOVING) for a in range(PASSES)]
        v_scales = sb("v_scales", [P, S], U8)
        v_planes = mx("v_planes", [P, PASSES, S], U8, 1, MOVING_SCALE)
        temp_rows = sb("temp_rows", [P, P], F32)
        c_words = mx("c_words", [P, S2], U32, 4, MOVING)
        c_plane = mx("c_plane", [P, S2], U8, 1, MOVING_SCALE)
        w1_bf = [sb("w1_bf%d" % a, [P, PACK * H], BF16) for a in range(PASSES)]
        w1_codes = [mx("w1_codes%d" % a, [P, H], U32, 4, STILL) for a in range(PASSES)]
        w1_planes = [mx("w1_planes%d" % a, [P, H], U8, 1, STILL_SCALE) for a in range(PASSES)]
        h_rows = [sb("h_rows%d" % half, [P, PACK, BANK], BF16) for half in range(HALVES)]
        h_woven = sb("h_woven", [P, TILES, P * PACK], BF16, tag="woven_then_relu")
        h_ps = [[bank("h_ps0_%d" % t, t) for t in range(PACK)]]
        sig = sb("sig", [P, TILES, S2], F32)
        ln = sb("ln", [P, TILES, S2], F32)
        z_ps = []

        def half_cols(half):
            return slice(BANK * half, BANK * (half + 1))

        def tile_cols(i):
            return slice(P * i, P * (i + 1))

        def live_rows(quad):
            return slice(32 * quad, 32 * quad + LIVE)

        def load_scale_rows(engine, plane, rows_of):
            for quad in range(QUADS):
                engine.dma_start(out=plane(live_rows(quad)), in_=rows_of(slice(LIVE * quad, LIVE * (quad + 1))).bitcast(I32))

        def load_w1(a, j0, j1):
            rows = w1[P * PACK * a : P * PACK * (a + 1), :].rearrange("(p j) c -> p j c", j=PACK)
            nc.sync.dma_start(out=w1_raw[a][:, j0:j1, :], in_=rows[:, j0:j1, :])

        def load_words(tile, words):
            nc.sync.dma_start(out=tile[:], in_=words.rearrange("p t i -> p (t i)").bitcast(I32))

        def gather_words(a, cols):
            picks = tokens[:, cols.start // LIST_ROWS : cols.stop // LIST_ROWS]
            nc.vector.tensor_copy(out=v_words[a][:, cols], in_=v_word_tab[a][:].bitcast(U32).indirect(picks))

        def move_scale_rows(a):
            for quad in range(QUADS):
                first = QUADS * LIVE * a + LIVE * quad
                nc.sync.dma_start(out=v_planes[live_rows(quad), a, :].bitcast(I32), in_=v_scales[first : first + LIVE, :].bitcast(I32))

        def round_w1(copy, a, c0, c1):
            copy(
                out=w1_bf[a][:].rearrange("p (t m j) -> p m t j", t=PACK, j=PACK)[:, c0 // PACK : c1 // PACK, :, :],
                in_=w1_raw[a][:, :, c0:c1].rearrange("p j (m t) -> p m t j", t=PACK),
            )

        def quantize_w1(a):
            round_w1(nc.scalar.copy, a, 0, SCALAR_SHARE)
            round_w1(nc.vector.tensor_copy, a, SCALAR_SHARE, H)
            nc.vector.quantize_mx(out=w1_codes[a][:].bitcast(FP8X4), scales=w1_planes[a][:], in_=w1_bf[a][:])

        def pass_w4(a, half, t, part=slice(0, BANK)):
            cols = slice(BANK * half + part.start, BANK * half + part.stop)
            nc.tensor.matmul_mx(
                out=h_ps[half][t][:, part],
                lhsT=w4_codes[:, a, 2 * P * t : 2 * P * (t + 1)].bitcast(FP4X4),
                lhsT_scale=w4_planes[:, a, tile_cols(t)],
                rhs=v_words[a][:, cols].bitcast(FP8X4),
                rhs_scale=v_planes[:, a, cols],
                start=(a == 0),
                stop=False,
            )

        def pass_w1(a, half, t, part=slice(0, BANK)):
            cols = slice(BANK * half + part.start, BANK * half + part.stop)
            nc.tensor.matmul_mx(
                out=h_ps[half][t][:, part],
                lhsT=w1_codes[a][:, tile_cols(t)].bitcast(FP8X4),
                lhsT_scale=w1_planes[a][:, tile_cols(t)],
                rhs=v_words[a][:, cols].bitcast(FP8X4),
                rhs_scale=v_planes[:, a, cols],
                start=False,
                stop=(a == PASSES - 1 and part.stop == BANK),
            )

        def score(i):
            half, sub = divmod(i, BANK // P)
            nc.vector.tensor_copy(
                out=h_woven[:, i, :].rearrange("p (c n t) -> p c t n", n=RUN, t=PACK),
                in_=h_rows[half][:, :, tile_cols(sub)].rearrange("p t (c n) -> p c t n", n=RUN),
            )
            h_codes = mx("h_codes%d" % i, [P, P], U32, 4, STILL)
            h_plane = mx("h_plane%d" % i, [P, P], U8, 1, STILL_SCALE)
            nc.vector.quantize_mx(out=h_codes[:].bitcast(FP8X4), scales=h_plane[:], in_=h_woven[:, i, :])
            z = bank("z_ps%d" % i, i)
            nc.tensor.matmul_mx(
                out=z[:],
                lhsT=h_codes[:].bitcast(FP8X4),
                lhsT_scale=h_plane[:],
                rhs=c_words[:].bitcast(FP8X4),
                rhs_scale=c_plane[:],
                start=True,
                stop=True,
            )
            nc.scalar.activation(out=sig[:, i, :], in_=z[:], func=ACT.Sigmoid, scale=neg_temp[:, i : i + 1])
            z_ps.append(z)

        nc.gpsimd.memset(warm[:], 0.0)
        nc.scalar.activation(out=warm[:, 1:2], in_=warm[:, 0:1], func=ACT.Sigmoid)
        nc.vector.memset(v_scale_tab[32:64, :], 0)
        nc.vector.memset(v_scale_tab[64:P, :], 0)
        nc.gpsimd.memset(w4_scale_raw[:], 0)
        nc.gpsimd.memset(temp_rows[:], 0.0)
        nc.gpsimd.memset(v_planes[:].bitcast(I32), 0)
        nc.gpsimd.memset(c_scale_tab[:], 0)
        make_identity(nc, ident[:])

        nc.sync.dma_start(out=v_scale_tab[0:32, :], in_=tab_scales.rearrange("a q t -> (a q) t").bitcast(I32))
        nc.sync.dma_start(tokens[:], offs)
        nc.sync.dma_start(out=w4_raw[:], in_=w4_words.rearrange("a p n -> p a n").bitcast(I32))
        load_words(v_word_tab[0], tab_words[0])
        load_w1(0, 0, PACK)
        load_w1(1, 0, AHEAD)
        load_scale_rows(nc.scalar, lambda live: w4_scale_raw[live, :, :], lambda rows: w4_scales[:, rows, :].rearrange("a r n -> r a n"))
        nc.scalar.dma_start(out=temp_rows[0:TILES, :], in_=temp.rearrange("(i p) -> i p", p=P))
        nc.vector.tensor_copy(out=v_scales[:], in_=v_scale_tab[:].bitcast(U8).indirect(tokens[:]))
        move_scale_rows(0)
        load_w1(1, AHEAD, PACK)
        load_words(v_word_tab[1], tab_words[1])
        nc.sync.dma_start(experts[:], offs2)
        move_scale_rows(1)
        load_words(c_word_tab, tab2_words[0])
        load_scale_rows(nc.sync, lambda live: c_scale_tab[live, :], lambda rows: tab2_scales[0, rows, :])
        nc.sync.dma_start(out=bias[:], in_=b1.rearrange("(p t) -> p t", t=PACK))

        nc.vector.tensor_copy(
            out=w4_codes[:].bitcast(U16).rearrange("p a (t m) -> p a t m", t=PACK),
            in_=w4_raw[:].bitcast(U16).rearrange("p a (m t) -> p a t m", t=PACK),
        )
        nc.vector.tensor_copy(
            out=w4_planes[:].rearrange("p a (t m) -> p a t m", t=PACK),
            in_=w4_scale_raw[:].bitcast(U8).rearrange("p a (m t) -> p a t m", t=PACK),
        )
        temp_ps = bank("temp_ps", TILES - 1)
        nc.tensor.transpose(temp_ps[:, 0:P], temp_rows[:], ident[:])
        nc.scalar.activation(out=neg_temp[:], in_=temp_ps[:, 0:TILES], func=ACT.Copy, scale=-1.0)
        warm_ps = bank("warm_ps", TILES - 2)
        for t in range(WARM_PASSES):
            nc.tensor.matmul_mx(
                out=warm_ps[:],
                lhsT=w4_raw[:, 0, P // 2 * t : P // 2 * (t + 1)].bitcast(U8).bitcast(FP4X4),
                lhsT_scale=w4_scale_raw[:, 0, :].bitcast(U8)[:, tile_cols(t)],
                rhs=v_word_tab[0][:, 0:BANK].bitcast(FP8X4),
                rhs_scale=w4_scale_raw[:, 1, :].bitcast(U8),
                start=True,
                stop=True,
            )
        h_ps.append([bank("h_ps1_%d" % t, PACK + t) for t in range(PACK)])

        for half in range(HALVES):
            gather_words(0, half_cols(half))
            for t in range(PACK):
                pass_w4(0, half, t)
        quantize_w1(0)
        for half in range(HALVES):
            for t in range(PACK):
                pass_w1(0, half, t)
        quantize_w1(1)
        gather_words(1, slice(0, PIECE))
        for t in range(SPLIT_BANKS):
            pass_w4(1, 0, t, slice(0, PIECE))
            pass_w1(1, 0, t, slice(0, PIECE))
        for half in range(HALVES):
            gather_words(1, slice(PIECE, BANK) if half == 0 else half_cols(half))
            for t in range(PACK):
                part = slice(PIECE if half == 0 and t < SPLIT_BANKS else 0, BANK)
                pass_w4(1, half, t, part)
                pass_w1(1, half, t, part)
                last = half == HALVES - 1 and t == PACK - 1
                cols = slice(0, BANK - VECTOR_TILES * P if last else BANK)
                nc.scalar.activation(out=h_rows[half][:, t, cols], in_=h_ps[half][t][:, cols], func=ACT.Identity, bias=bias[:, t : t + 1])

        nc.vector.tensor_copy(out=c_words[:], in_=c_word_tab[:].bitcast(U32).indirect(experts[:]))
        nc.vector.tensor_copy(out=c_plane[:], in_=c_scale_tab[:].bitcast(U8).indirect(experts[:]))
        for i in range(TILES):
            if i == TILES - VECTOR_TILES:
                cols = slice(BANK - VECTOR_TILES * P, BANK)
                nc.vector.tensor_scalar(
                    out=h_rows[-1][:, PACK - 1, cols], in0=h_ps[-1][-1][:, cols], scalar1=bias[:, PACK - 1 : PACK], scalar2=None, op0=ALU.add
                )
            score(i)

        ln_floor = sb("ln_floor", [P, 1], F32)
        nc.gpsimd.tensor_scalar(out=ln_floor[:], in0=sig[:, TILES - 2, 0:1], scalar1=0.0, scalar2=LN_FLOOR, op0=ALU.mult, op1=ALU.add)

        neg_relu = sb("neg_relu", [P, TILES, S2], F32, tag="woven_then_relu")
        for i in range(TILES):
            nc.vector.tensor_scalar(
                out=neg_relu[:, i, :], in0=z_ps[i][:], scalar1=neg_temp[:, i : i + 1], scalar2=-SQRT_FLOOR, op0=ALU.mult, op1=ALU.min
            )

        o_ps = [bank("o_ps%d" % b, b) for b in range(TILES)]
        neg_soft = []
        for i in range(TILES):
            if i % LN_TILES == 0:
                group = slice(i, i + LN_TILES)
                nc.scalar.activation(out=ln[:, group, :], in_=sig[:, group, :], func=ACT.Ln, bias=ln_floor[:])
            neg_soft.append(sb("neg_soft%d" % i, [P, S2], F32))
            nc.vector.tensor_tensor(out=neg_soft[i][:], in0=neg_relu[:, i, :], in1=ln[:, i, :], op=ALU.min)
            half, sub = divmod(i, BANK // P)
            for q in range(S2 // P):
                nc.tensor.transpose(o_ps[PACK * half + q][:, tile_cols(sub)], neg_soft[i][:, tile_cols(q)], ident[:])

        for b in range(TILES):
            half, q = divmod(b, S2 // P)
            cuts = [0, EDGE, BANK] if b == 0 else [0, BANK - EDGE, BANK] if b == TILES - 1 else [0, BANK]
            for c0, c1 in zip(cuts, cuts[1:]):
                res = sb("res%d_%d" % (b, c0), [P, c1 - c0], F32)
                nc.scalar.activation(out=res[:], in_=o_ps[b][:, c0:c1], func=ACT.Sqrt, scale=-1.0)
                nc.sync.dma_start(out=out[tile_cols(q), BANK * half + c0 : BANK * half + c1], in_=res[:])
